import numpy as np
import ml_dtypes


def mxq(x, axis, fmt="e4m3"):
    dtype, down = {"e4m3": (ml_dtypes.float8_e4m3fn, 7), "e5m2": (ml_dtypes.float8_e5m2, 14)}[fmt]
    v = np.moveaxis(np.asarray(x, np.float32).astype(ml_dtypes.bfloat16).astype(np.float64), axis, -1)
    blocks = v.reshape(v.shape[:-1] + (-1, 32))
    amax = np.abs(blocks).max(-1, keepdims=True)
    byte = np.maximum(np.where(amax > 0, np.frexp(amax)[1] - 1 + 127, 0) - down, 1)
    scale = np.exp2(byte - 127.0)
    codes = (blocks / scale).astype(np.float32).astype(dtype).astype(np.float64)
    return np.moveaxis((codes * scale).reshape(v.shape), -1, axis)


WIDE = False


def mx_kscale(k):
    if not WIDE:
        return np.ones(k)
    levels = np.array([10, -10, 5, -5, 0])
    if k % 512:
        return np.exp2(np.random.permutation(np.resize(levels, k // 32))).repeat(32)
    a = np.empty((k // 512, 16))
    for p in range(k // 512):
        a[p, :8] = np.random.permutation(np.resize(levels, 8))
        for g in range(8):
            far = levels[np.abs(levels - a[p, g]) >= 10]
            a[p, g + 8] = far[np.random.randint(len(far))]
    return np.exp2(a.ravel()).repeat(32)


BF16 = ml_dtypes.bfloat16


def bf(x):
    return np.asarray(x, np.float32).astype(BF16)


def f64(x):
    return np.asarray(x).astype(np.float64)


E2M1 = np.array([0.0, 0.5, 1.0, 1.5, 2.0, 3.0, 4.0, 6.0, -0.0, -0.5, -1.0, -1.5, -2.0, -3.0, -4.0, -6.0])


def pack_weight(w, fmt):
    k, n = w.shape
    w = f64(bf(w)).reshape(k // 32, 32, n)
    amax = np.abs(w).max(1)
    if fmt == "e4m3":
        byte = np.frexp(amax)[1] - 1 + 127 - 7
    else:
        mant, ex = np.frexp(amax / 6.0)
        byte = np.where(mant > 0.5, ex, ex - 1) + 127
    byte = np.clip(np.where(amax > 0, byte, 1), 1, 254)
    scaled = (w * np.exp2(127.0 - byte)[:, None, :]).reshape(k, n).astype(np.float32)
    by_word = np.ascontiguousarray(scaled.reshape(k // 512, 128, 4, n).transpose(0, 1, 3, 2))
    if fmt == "e4m3":
        words = by_word.astype(ml_dtypes.float8_e4m3fn).view(np.uint8)
    else:
        c = by_word.astype(ml_dtypes.float4_e2m1fn).view(np.uint8) & 0xF
        words = c[..., 0::2] | (c[..., 1::2] << 4)
    return np.ascontiguousarray(words), np.ascontiguousarray(byte.astype(np.uint8).reshape(k // 512, 16, n))


def unpack_weight(words, scales, fmt):
    g, p, n, _ = words.shape
    if fmt == "e4m3":
        vals = np.ascontiguousarray(words).view(ml_dtypes.float8_e4m3fn).astype(np.float64)
    else:
        nib = np.empty((g, p, n, 4), np.uint8)
        nib[..., 0::2] = words & 0xF
        nib[..., 1::2] = words >> 4
        vals = E2M1[nib]
    vals = vals * np.repeat(np.exp2(scales.astype(np.float64) - 127.0), 8, axis=1)[..., None]
    return vals.transpose(0, 1, 3, 2).reshape(g * 512, n)
def pack4(w):
    words, scales = pack_weight(w, "e2m1")
    return words.reshape(words.shape[0], 128, -1), scales


def unpack4(words, scales):
    return unpack_weight(words.reshape(words.shape[0], 128, -1, 2), scales, "e2m1")


def planes(Y):
    n, m = Y.shape
    b = f64(bf(Y)).reshape(n // 32, 32, m)
    amax = np.abs(b).max(1)
    byte = np.clip(np.where(amax > 0, np.frexp(amax)[1] - 1 + 127 - 7, 1), 1, 254)
    codes = (b * np.exp2(127.0 - byte)[:, None, :]).reshape(n, m).astype(np.float32).astype(ml_dtypes.float8_e4m3fn).view(np.uint8)
    words = codes.reshape(n // 512, 128, 4, m).transpose(0, 1, 3, 2)
    return np.ascontiguousarray(words), np.ascontiguousarray(byte.astype(np.uint8).reshape(n // 512, 16, m))


L, P, B, D, T = 3, 2, 1024, 1024, 512


def scaled_message(n):
    w = np.exp(n - n.max(-1, keepdims=True))
    return n.shape[-1] * (w / w.sum(-1, keepdims=True))


def log_normalise(q):
    top = q.max(-1, keepdims=True)
    log_z = top + np.log(np.sum(np.exp(q - top), axis=-1, keepdims=True))
    return q - log_z + np.log(q.shape[-1])


def setup_inputs():
    s = mx_kscale(D)
    t = np.stack([mx_kscale(T) for _ in range(P)])
    x = bf(np.random.standard_normal((L, B, D)) * s)
    words, scales = pack4(np.random.standard_normal((D, T)) / np.sqrt(D) / s[:, None])
    return {
        "x": x,
        "we_words": words,
        "we_scales": scales,
        "be": bf(0.3 * np.random.standard_normal(T)),
        "ends": bf(0.5 * np.random.standard_normal((P, T))),
        "gain": bf(np.random.standard_normal((P, T)) * t),
        "trans": bf(np.random.standard_normal((P, T, T)) * 3.5 / np.sqrt(T) / t[:, :, None]),
    }


def core(x, we_words, we_scales, be, ends, gain, trans):
    e = (mxq(f64(x), 2, "e4m3") @ unpack4(we_words, we_scales)) + f64(be)
    en = f64(ends)
    n = np.stack([e[0] + en[0], e[2] + en[1]], axis=0)
    u = scaled_message(n)
    v = u * f64(gain)[:, None, :]
    m = mxq(v, 2, "e4m3") @ mxq(f64(trans), 1, "e4m3")
    c = np.log(np.maximum(1.0 + m / 16.0, 0.1))
    q = e[1] + c[0] + c[1]
    return log_normalise(q)


def reference(x, we_words, we_scales, be, ends, gain, trans):
    R_out = core(x, we_words, we_scales, be, ends, gain, trans)
    words, scales = planes(R_out.T)
    return R_out, words, scales

@@ -1,0 +1,497 @@
+from contextlib import ExitStack
+
+import concourse.mybir as mybir
+from concourse.masks import make_identity
+
+F32 = mybir.dt.float32
+BF16 = mybir.dt.bfloat16
+I32 = mybir.dt.int32
+U32 = mybir.dt.uint32
+U8 = mybir.dt.uint8
+FP8X4 = mybir.dt.float8_e4m3fn_x4
+FP4X4 = mybir.dt.float4_e2m1fn_x4
+ALU = mybir.AluOpType
+ACT = mybir.ActivationFunctionType
+AX = mybir.AxisListType
+
+LAYERS, TOKENS, D, T = 3, 1024, 1024, 512
+P = 128
+CHUNKS = TOKENS // P
+G = D // 512
+FLOPS = 2 * LAYERS * TOKENS * D * T + 2 * 2 * TOKENS * T * T
+MANUAL = True
+LORD = (0, 2, 1)
+TR = ()
+VG = ()
+EZG = ()
+VXC = ()
+VRC = ()
+GSPLIT = 1
+TE = "G"
+TPARTS = 2
+EB = 3
+XB = 2
+VB = 1
+MB = 2
+TB = 1
+VCE = "S"
+ORDER = [
+    ("zA", "c", 23),
+    ("zR", "c", 12),
+    ("xT", "u", 0),
+    ("eM", "u", 2),
+    ("xC", "u", 0),
+    ("rC", "t", 32),
+    ("vR", "c", 5),
+    ("kG", "g", 5),
+    ("vM1", "c", 6),
+    ("eN", "u", 2),
+    ("xQ", "u", 0),
+    ("vT", "c", 6),
+    ("rA", "t", 28),
+    ("f1", "c", 9),
+    ("eE", "u", 3),
+    ("vM0", "c", 5),
+    ("eX", "u", 2),
+    ("rT", "t", 29),
+    ("rL", "t", 27),
+    ("f0", "c", 9),
+    ("tQ", "q", 5),
+    ("vG0", "c", 4),
+    ("rQ", "t", 32),
+    ("kB", "k", 0),
+    ("mM", "c", 8),
+    ("tI", "i", 2),
+    ("vG1", "c", 13),
+    ("zP", "c", 10),
+    ("vQ", "c", 7),
+    ("zE", "c", 10),
+    ("vC", "c", 6),
+]
+
+
+def tile_chunkflooredmessagemiddlescore_kernel(
+    tc, x, we_words, we_scales, be, ends, gain, trans, out_0, out_1, out_2
+):
+    nc = tc.nc
+    with ExitStack() as ctx:
+        keep = ctx.enter_context(tc.tile_pool(name="keep", bufs=1))
+        work = ctx.enter_context(tc.tile_pool(name="work", bufs=3))
+        psum = ctx.enter_context(tc.psum_pool(name="psum", bufs=2))
+        if MANUAL:
+            ctx.enter_context(tc.manual_schedule())
+
+        xs = {}
+
+        def load_x(c, layer):
+            t = keep.tile([P, D], BF16, name=f"x_{c}_{layer}", align_bytes=64)
+            nc.sync.dma_start(out=t[:], in_=x[layer, c * P : (c + 1) * P, :])
+            xs[c, layer] = t
+
+        we = keep.tile([P, G, 2 * T], U8, name="we", align_bytes=64)
+        wscale = keep.tile([P, G, T], U8, name="wscale", align_bytes=64)
+        rows = keep.tile([P, 5, T], BF16, name="rows", align_bytes=64)
+        ones = keep.tile([P, P], BF16, name="ones", align_bytes=64)
+        ident = keep.tile([P, P], F32, name="ident")
+        make_identity(nc, ident[:])
+        nc.vector.memset(wscale[:].rearrange("p g n -> p (g n)").bitcast(I32), 0)
+        nc.vector.memset(rows[:], 0.0)
+        nc.vector.memset(ones[:], 1.0)
+        load_x(0, LORD[0])
+        nc.sync.dma_start(
+            out=we[:].rearrange("p g n -> p (g n)").bitcast(I32).rearrange("p (g n) -> p g n", g=G),
+            in_=we_words.bitcast(I32).rearrange("g p n -> p g n"),
+        )
+        for q in range(4):
+            nc.scalar.dma_start(
+                out=wscale[32 * q : 32 * q + 4, :, :].rearrange("p g n -> p (g n)").bitcast(I32).rearrange("p (g n) -> p g n", g=G),
+                in_=we_scales[:, 4 * q : 4 * q + 4, :].bitcast(I32).rearrange("g r n -> r g n"),
+            )
+        nc.scalar.dma_start(out=rows[0:1, 0, :], in_=be.unsqueeze(0))
+        nc.scalar.dma_start(out=rows[0:1, 1:3, :], in_=ends.unsqueeze(0))
+        nc.scalar.dma_start(out=rows[0:1, 3:5, :], in_=gain.unsqueeze(0))
+        load_x(0, LORD[1])
+        load_x(0, LORD[2])
+        for layer in LORD:
+            load_x(1, layer)
+        traw = []
+        for p in range(2):
+            t = keep.tile([P, 4, T], BF16, name=f"traw_{p}", align_bytes=64)
+            nc.sync.dma_start(out=t[:], in_=trans[p].rearrange("(k j) n -> k j n", j=4))
+            traw.append(t)
+        for c in range(2, CHUNKS):
+            for layer in LORD:
+                load_x(c, layer)
+        warm = keep.tile([P, 1], F32, name="warm")
+        nc.vector.memset(warm[:], 0.0)
+        nc.scalar.activation(out=warm[:], in_=warm[:], func=ACT.Exp)
+
+        st = {}
+        stats = {}
+        for c in range(CHUNKS):
+            s = keep.tile([P, 16], F32, name=f"stats_{c}")
+            stats[c] = s
+        units = [(c, layer) for c in range(CHUNKS) for layer in LORD]
+        BROW = {0: 1, 2: 2, 1: None}
+        bias, bcol, gain512 = {}, {}, {}
+
+        def kB(i):
+            layer = LORD[i]
+            row = BROW[layer]
+            acc = psum.tile([P, T], F32, name="acc", tag="e", bufs=EB)
+            if layer in TR:
+                for j in range(4):
+                    cols = slice(P * j, P * (j + 1))
+                    o = acc[:, 2 * j : 2 * j + 2]
+                    nc.tensor.matmul(o, lhsT=rows[:, 0, cols], rhs=ones[:, 0:2], start=True, stop=row is None)
+                    if row is not None:
+                        nc.tensor.matmul(o, lhsT=rows[:, row, cols], rhs=ones[:, 0:2], start=False, stop=True)
+                b = keep.tile([P, 8], F32, name=f"bcol_{layer}")
+                nc.scalar.copy(out=b[:], in_=acc[:, 0:8])
+                bcol[layer] = b
+            else:
+                nc.tensor.matmul(acc[:], lhsT=ones[:], rhs=rows[:, 0, :], start=True, stop=row is None)
+                if row is not None:
+                    nc.tensor.matmul(acc[:], lhsT=ones[:], rhs=rows[:, row, :], start=False, stop=True)
+                b = keep.tile([P, T], F32, name=f"bias_{layer}")
+                nc.scalar.copy(out=b[:], in_=acc[:])
+                bias[layer] = b
+
+        def kG(p):
+            acc = psum.tile([P, T], F32, name="acc", tag="m", bufs=MB)
+            nc.tensor.matmul(acc[:], lhsT=ones[:], rhs=rows[:, 3 + p, :], start=True, stop=True)
+            g = keep.tile([P, T], F32, name=f"gain_{p}")
+            nc.scalar.activation(out=g[:], in_=acc[:], func=ACT.Copy, scale=512.0)
+            gain512[p] = g
+
+        tcodes = keep.tile([P, 2, T], U32, name="tcodes", align_bytes=64)
+        tscale = keep.tile([P, 2, T], U8, name="tscale", align_bytes=64)
+        tgrp = []
+        for p in range(2):
+            t = keep.tile([P, T, 4], BF16, name=f"tgrp_{p}", align_bytes=64)
+            tgrp.append(t)
+
+        def tI(i):
+            p, part = divmod(i, TPARTS)
+            n = slice(part * T // TPARTS, (part + 1) * T // TPARTS)
+            src = traw[p][:, :, n].rearrange("k j n -> k n j")
+            if TE == "G":
+                nc.gpsimd.tensor_scalar(
+                    out=tgrp[p][:, n, :], in0=src, scalar1=1.0, scalar2=1.0, op0=ALU.mult, op1=ALU.mult
+                )
+            elif TE == "V":
+                nc.vector.tensor_copy(out=tgrp[p][:, n, :], in_=src)
+            else:
+                nc.scalar.copy(out=tgrp[p][:, n, :], in_=src)
+
+        def tQ(p):
+            nc.vector.quantize_mx(
+                out=tcodes[:, p, :].bitcast(FP8X4), scales=tscale[:, p, :],
+                in_=tgrp[p][:].rearrange("k n j -> k (n j)"),
+            )
+
+        def xT(s):
+            u = units[s]
+            xt = psum.tile([P, G, 2, P], F32, name="xt", tag="xt", bufs=XB)
+            w = xs[u][:].bitcast(F32)
+            for g in range(G):
+                for h in range(2):
+                    nc.tensor.transpose(xt[:, g, h, :], w[:, 256 * g + h : 256 * (g + 1) : 2], ident[:])
+            st["xt", u] = xt
+
+        def xC(s):
+            u = units[s]
+            xg = work.tile([P, G * P * 4], BF16, name="xg", tag="xg", bufs=3, align_bytes=64)
+            eng = nc.vector.tensor_copy if s in VXC else nc.scalar.copy
+            eng(
+                out=xg[:].bitcast(F32).rearrange("p (g r h) -> p g r h", g=G, h=2),
+                in_=st.pop(("xt", u))[:].rearrange("p g h r -> p g r h"),
+            )
+            st["xg", u] = xg
+
+        def xQ(s):
+            u = units[s]
+            xq = work.tile([P, G, P], U32, name="xq", tag="xq", bufs=3, align_bytes=64)
+            xsc = work.tile([P, G, P], U8, name="xsc", tag="xsc", bufs=3, align_bytes=64)
+            nc.vector.quantize_mx(
+                out=xq[:].rearrange("p g r -> p (g r)").bitcast(FP8X4),
+                scales=xsc[:].rearrange("p g r -> p (g r)"),
+                in_=st.pop(("xg", u))[:],
+            )
+            st["xq", u] = (xq, xsc)
+
+        def eM(s):
+            u = units[s]
+            xq, xsc = st.pop(("xq", u))
+            if u[1] in TR:
+                acc = psum.tile([P, 4, P], F32, name="et", tag="et", bufs=TB)
+                for j in range(4):
+                    for g in range(G):
+                        nc.tensor.matmul_mx(
+                            out=acc[:, j, :],
+                            lhsT=we[:, g, 2 * P * j : 2 * P * (j + 1)].bitcast(FP4X4),
+                            lhsT_scale=wscale[:, g, P * j : P * (j + 1)],
+                            rhs=xq[:, g, :].bitcast(FP8X4), rhs_scale=xsc[:, g, :],
+                            start=g == 0, stop=g == G - 1,
+                        )
+                st["et", u] = acc
+            else:
+                acc = psum.tile([P, T], F32, name="e", tag="e", bufs=EB)
+                for g in range(G):
+                    nc.tensor.matmul_mx(
+                        out=acc[:],
+                        lhsT=xq[:, g, :].bitcast(FP8X4), lhsT_scale=xsc[:, g, :],
+                        rhs=we[:, g, :].bitcast(FP4X4), rhs_scale=wscale[:, g, :],
+                        start=g == 0, stop=g == G - 1,
+                    )
+                st["e", u] = acc
+
+        def eS(s):
+            u = units[s]
+            if u[1] not in TR:
+                return
+            et = st.pop(("et", u))
+            es = work.tile([P, 4, P], F32, name="es", tag="es", bufs=2)
+            for j in range(4):
+                nc.scalar.activation(out=es[:, j, :], in_=et[:, j, :], func=ACT.Identity, bias=bcol[u[1]][:, 2 * j : 2 * j + 1], scale=1.0)
+            st["es", u] = es
+
+        def eT(s):
+            u = units[s]
+            if u[1] not in TR:
+                return
+            es = st.pop(("es", u))
+            acc = psum.tile([P, T], F32, name="e", tag="e", bufs=EB)
+            for j in range(4):
+                nc.tensor.transpose(acc[:, P * j : P * (j + 1)], es[:, j, :], ident[:])
+            st["e", u] = acc
+
+        def eN(s):
+            u = units[s]
+            c, layer = u
+            if layer in TR:
+                return
+            if layer == 1:
+                n = keep.tile([P, T], F32, name=f"e1_{c}")
+            else:
+                n = work.tile([P, T], F32, name="n", tag="n", bufs=3)
+            nc.vector.tensor_tensor(out=n[:], in0=st.pop(("e", u))[:], in1=bias[layer][:], op=ALU.add)
+            st["n", u] = n
+
+        def eX(s):
+            c, layer = units[s]
+            u = units[s]
+            if layer in TR and layer == 1:
+                n = keep.tile([P, T], F32, name=f"e1_{c}")
+                nc.vector.tensor_scalar(
+                    out=n[:], in0=st.pop(("e", u))[:], scalar1=-1.0, scalar2=None, op0=ALU.mult, op1=ALU.min,
+                    accum_out=stats[c][:, 1:2],
+                )
+                st["n", u] = n
+                return
+            if layer in TR:
+                st["n", u] = st.pop(("e", u))
+            nc.vector.tensor_reduce(
+                out=stats[c][:, layer : layer + 1], in_=st["n", u][:], axis=AX.X, op=ALU.max, negate=True
+            )
+
+        def eE(s):
+            u = units[s]
+            c, layer = u
+            ex = work.tile([P, T], F32, name="ex", tag=f"ex{layer}", bufs=3)
+            n = st["n", u]
+            if layer == 1:
+                nc.scalar.activation(
+                    out=ex[:], in_=n[:], func=ACT.Exp, bias=stats[c][:, 1:2], scale=-1.0 if 1 in TR else 1.0
+                )
+            else:
+                st.pop(("n", u))
+                nc.scalar.activation(
+                    out=ex[:], in_=n[:], func=ACT.Exp, bias=stats[c][:, layer : layer + 1], scale=1.0,
+                    accum_out=stats[c][:, 4 + layer // 2 : 5 + layer // 2],
+                )
+            st["ex", u] = ex
+
+        def vR(c):
+            s = stats[c]
+            nc.vector.reciprocal(out=s[:, 8:10], in_=s[:, 4:6])
+
+        def vG(c, p):
+            if 2 * c + p not in VG:
+                return
+            gx = work.tile([P, T], F32, name="gx", tag=f"gx{p}", bufs=2)
+            ex = st.pop(("ex", (c, 2 * p)))
+            for a in range(GSPLIT):
+                k = slice(a * T // GSPLIT, (a + 1) * T // GSPLIT)
+                nc.gpsimd.tensor_tensor(out=gx[:, k], in0=ex[:, k], in1=gain512[p][:, k], op=ALU.mult)
+            st["gx", c, p] = gx
+
+        def vM(c, p):
+            v = work.tile([P, T], BF16, name="v", tag=f"v{p}", bufs=2, align_bytes=64)
+            if 2 * c + p in VG:
+                nc.scalar.activation(
+                    out=v[:], in_=st.pop(("gx", c, p))[:], func=ACT.Copy, scale=stats[c][:, 8 + p : 9 + p]
+                )
+            else:
+                nc.vector.scalar_tensor_tensor(
+                    out=v[:], in0=st.pop(("ex", (c, 2 * p)))[:], scalar=stats[c][:, 8 + p : 9 + p], in1=gain512[p][:],
+                    op0=ALU.mult, op1=ALU.mult,
+                )
+            st["v", c, p] = v
+
+        def vT(c):
+            vt = psum.tile([P, 2, 2, P], F32, name="vt", tag="vt", bufs=VB)
+            for p in range(2):
+                w = st.pop(("v", c, p))[:].bitcast(F32)
+                for h in range(2):
+                    nc.tensor.transpose(vt[:, p, h, :], w[:, h::2], ident[:])
+            st["vt", c] = vt
+
+        def vC(c):
+            vg = work.tile([P, 2 * P * 4], BF16, name="vg", tag="vg", bufs=2, align_bytes=64)
+            eng = nc.scalar.copy if VCE == "S" else nc.vector.tensor_copy
+            eng(
+                out=vg[:].bitcast(F32).rearrange("p (g r h) -> p g r h", g=2, h=2),
+                in_=st.pop(("vt", c))[:].rearrange("p g h r -> p g r h"),
+            )
+            st["vg", c] = vg
+
+        def vQ(c):
+            vq = work.tile([P, 2, P], U32, name="vq", tag="vq", bufs=2, align_bytes=64)
+            vsc = work.tile([P, 2, P], U8, name="vsc", tag="vsc", bufs=2, align_bytes=64)
+            nc.vector.quantize_mx(
+                out=vq[:].rearrange("p g r -> p (g r)").bitcast(FP8X4),
+                scales=vsc[:].rearrange("p g r -> p (g r)"),
+                in_=st.pop(("vg", c))[:],
+            )
+            st["vq", c] = (vq, vsc)
+
+        def mM(c):
+            vq, vsc = st.pop(("vq", c))
+            for p in range(2):
+                acc = psum.tile([P, T], F32, name="m", tag="m", bufs=MB)
+                nc.tensor.matmul_mx(
+                    out=acc[:],
+                    lhsT=vq[:, p, :].bitcast(FP8X4), lhsT_scale=vsc[:, p, :],
+                    rhs=tcodes[:, p, :].bitcast(FP8X4), rhs_scale=tscale[:, p, :],
+                    start=True, stop=True,
+                )
+                st["m", c, p] = acc
+
+        def f0(c):
+            r0 = work.tile([P, T], F32, name="r0", tag="r0", bufs=2)
+            nc.scalar.activation(out=r0[:], in_=st.pop(("m", c, 0))[:], func=ACT.Relu, bias=14.4, scale=1.0)
+            st["r0", c] = r0
+
+        def f1(c):
+            z1 = work.tile([P, T], F32, name="z1", tag="z1", bufs=2)
+            nc.vector.tensor_scalar(
+                out=z1[:], in0=st.pop(("m", c, 1))[:], scalar1=-14.4, scalar2=16.0, op0=ALU.max, op1=ALU.add
+            )
+            st["z1", c] = z1
+
+        def zP(c):
+            z = keep.tile([P, T], F32, name=f"z_{c}")
+            nc.vector.scalar_tensor_tensor(
+                out=z[:], in0=st.pop(("r0", c))[:], scalar=1.6, in1=st.pop(("z1", c))[:], op0=ALU.add, op1=ALU.mult
+            )
+            st["z", c] = z
+
+        def zE(c):
+            s = stats[c]
+            ez = work.tile([P, T], F32, name="ez", tag="ez", bufs=2)
+            ex = st.pop(("ex", (c, 1)))
+            if c in EZG:
+                for a in range(GSPLIT):
+                    k = slice(a * T // GSPLIT, (a + 1) * T // GSPLIT)
+                    nc.gpsimd.tensor_tensor(out=ez[:, k], in0=ex[:, k], in1=st["z", c][:, k], op=ALU.mult)
+                st["ez", c] = ez
+            else:
+                nc.vector.scalar_tensor_tensor(
+                    out=ez[:], in0=ex[:], scalar=1.0 / 512, in1=st["z", c][:],
+                    op0=ALU.mult, op1=ALU.mult, accum_out=s[:, 10:11],
+                )
+
+        def zA(c):
+            if c in EZG:
+                ez = st.pop(("ez", c))
+                nc.scalar.activation(
+                    out=ez[:], in_=ez[:], func=ACT.Copy, scale=1.0 / 512, accum_out=stats[c][:, 10:11]
+                )
+
+        def zR(c):
+            s = stats[c]
+            nc.vector.reciprocal(out=s[:, 11:12], in_=s[:, 10:11])
+
+        rcodes = keep.tile([P, TOKENS], U32, name="rcodes", align_bytes=64)
+        rscale = keep.tile([P, TOKENS], U8, name="rscale", align_bytes=64)
+
+        def rL(c):
+            lz = work.tile([P, T], F32, name="lz", tag="lz", bufs=3)
+            nc.scalar.activation(out=lz[:], in_=st.pop(("z", c))[:], func=ACT.Ln, scale=stats[c][:, 11:12])
+            st["lz", c] = lz
+
+        def rA(c):
+            r = work.tile([P, T], F32, name="r", tag="r", bufs=4)
+            n, lz = st.pop(("n", (c, 1))), st.pop(("lz", c))
+            if 1 in TR:
+                nc.vector.scalar_tensor_tensor(
+                    out=r[:], in0=lz[:], scalar=stats[c][:, 1:2], in1=n[:], op0=ALU.add, op1=ALU.subtract
+                )
+            else:
+                nc.vector.scalar_tensor_tensor(
+                    out=r[:], in0=n[:], scalar=stats[c][:, 1:2], in1=lz[:], op0=ALU.add, op1=ALU.add
+                )
+            nc.sync.dma_start(out=out_0[c * P : (c + 1) * P, :], in_=r[:])
+            st["r", c] = r
+
+        def rT(c):
+            rt = psum.tile([P, 4, P], F32, name="rt", tag="xt", bufs=XB)
+            r = st.pop(("r", c))
+            for j in range(4):
+                nc.tensor.transpose(rt[:, j, :], r[:, j::4], ident[:])
+            st["rt", c] = rt
+
+        def rC(c):
+            if c % 2 == 0:
+                rg = work.tile([P, 2, P, 4], BF16, name="rg", tag="rg", bufs=2, align_bytes=64)
+                st["rg", c // 2] = rg
+            eng = nc.vector.tensor_copy if c in VRC else nc.scalar.copy
+            eng(out=st["rg", c // 2][:, c % 2, :, :], in_=st.pop(("rt", c))[:].rearrange("p j r -> p r j"))
+
+        def rQ(c):
+            if c % 2 == 0:
+                return
+            k = c // 2
+            cols = slice(2 * P * k, 2 * P * (k + 1))
+            nc.vector.quantize_mx(
+                out=rcodes[:, cols].bitcast(FP8X4), scales=rscale[:, cols],
+                in_=st.pop(("rg", k))[:].rearrange("p c r j -> p (c r j)"),
+            )
+            nc.sync.dma_start(
+                out=out_1[0, :, cols, :].rearrange("p m t -> p (m t)").bitcast(I32), in_=rcodes[:, cols].bitcast(I32)
+            )
+
+        v0 = lambda f: (lambda c: f(c, 0))
+        v1 = lambda f: (lambda c: f(c, 1))
+        ops = {
+            "kB": kB, "kG": kG, "tI": tI, "tQ": tQ, "xT": xT, "xC": xC, "xQ": xQ, "eM": eM, "eS": eS, "eT": eT,
+            "eN": eN, "eX": eX, "eE": eE, "vR": vR, "vG0": v0(vG), "vG1": v1(vG), "vM0": v0(vM), "vM1": v1(vM),
+            "vT": vT, "vC": vC, "vQ": vQ, "mM": mM, "f0": f0, "f1": f1, "zP": zP, "zE": zE, "zA": zA, "zR": zR,
+            "rL": rL, "rA": rA, "rT": rT, "rC": rC, "rQ": rQ,
+        }
+        count = {"u": len(units), "c": CHUNKS, "t": CHUNKS, "k": 3, "g": 2, "i": 2 * TPARTS, "q": 2}
+        for s in range(60):
+            for op, kind, lag in ORDER:
+                j = s - lag
+                if kind == "c":
+                    if j % 3:
+                        continue
+                    j = j // 3
+                if 0 <= j < count[kind]:
+                    ops[op](j)
+        for q in range(4):
+            nc.sync.dma_start(
+                out=out_2[0, 4 * q : 4 * q + 4, :].bitcast(I32),
+                in_=rscale[32 * q : 32 * q + 4, :].bitcast(I32),
+            )

@@ -23,9 +23,9 @@ MANUAL = True
 LORD = (0, 2, 1)
 TR = ()
 VG = ()
-EZG = ()
+EZG = (0, 1, 2, 3, 4, 5)
 VXC = ()
-VRC = ()
+VRC = (1, 3, 5, 7)
 GSPLIT = 1
 TE = "G"
 TPARTS = 2
@@ -36,38 +36,45 @@ MB = 2
 TB = 1
 VCE = "S"
 ORDER = [
-    ("zA", "c", 23),
-    ("zR", "c", 12),
-    ("xT", "u", 0),
-    ("eM", "u", 2),
-    ("xC", "u", 0),
-    ("rC", "t", 32),
-    ("vR", "c", 5),
-    ("kG", "g", 5),
-    ("vM1", "c", 6),
+    ("mM", "c", 9),
+    ("vG0", "c", 5),
     ("eN", "u", 2),
-    ("xQ", "u", 0),
-    ("vT", "c", 6),
-    ("rA", "t", 28),
-    ("f1", "c", 9),
+    ("xQ", "u", 1),
+    ("zE", "c", 12),
+    ("kG1", "k", 3),
+    ("kG0", "k", 2),
+    ("zA", "c", 13),
+    ("f0", "c", 10),
+    ("vM1", "c", 6),
+    ("zR", "c", 13),
+    ("vG1", "c", 10),
+    ("vQ", "c", 8),
+    ("vT", "c", 7),
     ("eE", "u", 3),
-    ("vM0", "c", 5),
+    ("tQ", "q", 6),
     ("eX", "u", 2),
-    ("rT", "t", 29),
+    ("vR", "c", 4),
+    ("rC", "t", 31),
+    ("kB0", "k", 1),
+    ("kB2", "k", 2),
+    ("rA", "t", 28),
+    ("vM0", "c", 5),
+    ("kB1", "k", 1),
+    ("tI", "i", 3),
+    ("xT", "u", 0),
+    ("eM", "u", 1),
+    ("vC", "c", 7),
     ("rL", "t", 27),
-    ("f0", "c", 9),
-    ("tQ", "q", 5),
-    ("vG0", "c", 4),
-    ("rQ", "t", 32),
-    ("kB", "k", 0),
-    ("mM", "c", 8),
-    ("tI", "i", 2),
-    ("vG1", "c", 13),
+    ("rQ", "t", 34),
     ("zP", "c", 10),
-    ("vQ", "c", 7),
-    ("zE", "c", 10),
-    ("vC", "c", 6),
+    ("f1", "c", 9),
+    ("rT", "t", 30),
+    ("xC", "u", 0),
 ]
+DUM = 0
+ZG = ()
+W = (0, 1, 2, 3, 4, 5, 6)
+KBV = (0, 1, 2)
 
 
 def tile_chunkflooredmessagemiddlescore_kernel(
@@ -94,21 +101,22 @@ def tile_chunkflooredmessagemiddlescore_kernel(
         ones = keep.tile([P, P], BF16, name="ones", align_bytes=64)
         ident = keep.tile([P, P], F32, name="ident")
         make_identity(nc, ident[:])
+        nc.vector.memset(rows[:, 0:3, :], 0.0)
         nc.vector.memset(wscale[:].rearrange("p g n -> p (g n)").bitcast(I32), 0)
-        nc.vector.memset(rows[:], 0.0)
         nc.vector.memset(ones[:], 1.0)
+        nc.vector.memset(rows[:, 3:5, :], 0.0)
         load_x(0, LORD[0])
         nc.sync.dma_start(
             out=we[:].rearrange("p g n -> p (g n)").bitcast(I32).rearrange("p (g n) -> p g n", g=G),
             in_=we_words.bitcast(I32).rearrange("g p n -> p g n"),
         )
         for q in range(4):
-            nc.scalar.dma_start(
+            nc.sync.dma_start(
                 out=wscale[32 * q : 32 * q + 4, :, :].rearrange("p g n -> p (g n)").bitcast(I32).rearrange("p (g n) -> p g n", g=G),
                 in_=we_scales[:, 4 * q : 4 * q + 4, :].bitcast(I32).rearrange("g r n -> r g n"),
             )
-        nc.scalar.dma_start(out=rows[0:1, 0, :], in_=be.unsqueeze(0))
-        nc.scalar.dma_start(out=rows[0:1, 1:3, :], in_=ends.unsqueeze(0))
+        nc.scalar.dma_start(out=rows[0:1, 0:3, :], in_=be.unsqueeze(0).unsqueeze(0).to_broadcast([1, 3, T]))
+        nc.scalar.dma_start(out=rows[1:2, 0:2, :], in_=ends.unsqueeze(0))
         nc.scalar.dma_start(out=rows[0:1, 3:5, :], in_=gain.unsqueeze(0))
         load_x(0, LORD[1])
         load_x(0, LORD[2])
@@ -132,30 +140,18 @@ def tile_chunkflooredmessagemiddlescore_kernel(
             s = keep.tile([P, 16], F32, name=f"stats_{c}")
             stats[c] = s
         units = [(c, layer) for c in range(CHUNKS) for layer in LORD]
-        BROW = {0: 1, 2: 2, 1: None}
+        BROW = {0: 0, 2: 1, 1: 2}
         bias, bcol, gain512 = {}, {}, {}
 
         def kB(i):
             layer = LORD[i]
             row = BROW[layer]
             acc = psum.tile([P, T], F32, name="acc", tag="e", bufs=EB)
-            if layer in TR:
-                for j in range(4):
-                    cols = slice(P * j, P * (j + 1))
-                    o = acc[:, 2 * j : 2 * j + 2]
-                    nc.tensor.matmul(o, lhsT=rows[:, 0, cols], rhs=ones[:, 0:2], start=True, stop=row is None)
-                    if row is not None:
-                        nc.tensor.matmul(o, lhsT=rows[:, row, cols], rhs=ones[:, 0:2], start=False, stop=True)
-                b = keep.tile([P, 8], F32, name=f"bcol_{layer}")
-                nc.scalar.copy(out=b[:], in_=acc[:, 0:8])
-                bcol[layer] = b
-            else:
-                nc.tensor.matmul(acc[:], lhsT=ones[:], rhs=rows[:, 0, :], start=True, stop=row is None)
-                if row is not None:
-                    nc.tensor.matmul(acc[:], lhsT=ones[:], rhs=rows[:, row, :], start=False, stop=True)
-                b = keep.tile([P, T], F32, name=f"bias_{layer}")
-                nc.scalar.copy(out=b[:], in_=acc[:])
-                bias[layer] = b
+            nc.tensor.matmul(acc[:], lhsT=ones[:], rhs=rows[:, row, :], start=True, stop=True)
+            b = keep.tile([P, T], F32, name=f"bias_{layer}")
+            eng = nc.vector.tensor_copy if i in KBV else nc.scalar.copy
+            eng(out=b[:], in_=acc[:])
+            bias[layer] = b
 
         def kG(p):
             acc = psum.tile([P, T], F32, name="acc", tag="m", bufs=MB)
@@ -220,11 +216,21 @@ def tile_chunkflooredmessagemiddlescore_kernel(
             )
             st["xq", u] = (xq, xsc)
 
+        def warm_pass(acc, xq, xsc):
+            for g in range(DUM):
+                nc.tensor.matmul_mx(
+                    out=acc[:],
+                    lhsT=xq[:, g, :].bitcast(FP8X4), lhsT_scale=xsc[:, g, :],
+                    rhs=we[:, g, :].bitcast(FP4X4), rhs_scale=wscale[:, g, :],
+                    start=True, stop=True,
+                )
+
         def eM(s):
             u = units[s]
             xq, xsc = st.pop(("xq", u))
             if u[1] in TR:
                 acc = psum.tile([P, 4, P], F32, name="et", tag="et", bufs=TB)
+                warm_pass(acc[:].rearrange("p j n -> p (j n)"), xq, xsc)
                 for j in range(4):
                     for g in range(G):
                         nc.tensor.matmul_mx(
@@ -237,6 +243,7 @@ def tile_chunkflooredmessagemiddlescore_kernel(
                 st["et", u] = acc
             else:
                 acc = psum.tile([P, T], F32, name="e", tag="e", bufs=EB)
+                warm_pass(acc, xq, xsc)
                 for g in range(G):
                     nc.tensor.matmul_mx(
                         out=acc[:],
@@ -380,11 +387,27 @@ def tile_chunkflooredmessagemiddlescore_kernel(
 
         def f0(c):
             r0 = work.tile([P, T], F32, name="r0", tag="r0", bufs=2)
+            if c in ZG:
+                nc.vector.tensor_scalar(
+                    out=r0[:], in0=st.pop(("m", c, 0))[:], scalar1=-14.4, scalar2=16.0, op0=ALU.max, op1=ALU.add
+                )
+                st["r0", c] = r0
+                return
             nc.scalar.activation(out=r0[:], in_=st.pop(("m", c, 0))[:], func=ACT.Relu, bias=14.4, scale=1.0)
             st["r0", c] = r0
 
         def f1(c):
             z1 = work.tile([P, T], F32, name="z1", tag="z1", bufs=2)
+            if c in W:
+                r1 = work.tile([P, T], F32, name="r1", tag="r1", bufs=2)
+                nc.scalar.activation(out=r1[:], in_=st.pop(("m", c, 1))[:], func=ACT.Relu, bias=14.4, scale=1.0)
+                for a in range(GSPLIT):
+                    k = slice(a * T // GSPLIT, (a + 1) * T // GSPLIT)
+                    nc.gpsimd.tensor_scalar(
+                        out=z1[:, k], in0=r1[:, k], scalar1=1.6, scalar2=1.0, op0=ALU.add, op1=ALU.mult
+                    )
+                st["z1", c] = z1
+                return
             nc.vector.tensor_scalar(
                 out=z1[:], in0=st.pop(("m", c, 1))[:], scalar1=-14.4, scalar2=16.0, op0=ALU.max, op1=ALU.add
             )
@@ -392,6 +415,10 @@ def tile_chunkflooredmessagemiddlescore_kernel(
 
         def zP(c):
             z = keep.tile([P, T], F32, name=f"z_{c}")
+            if c in ZG:
+                nc.gpsimd.tensor_tensor(out=z[:], in0=st.pop(("r0", c))[:], in1=st.pop(("z1", c))[:], op=ALU.mult)
+                st["z", c] = z
+                return
             nc.vector.scalar_tensor_tensor(
                 out=z[:], in0=st.pop(("r0", c))[:], scalar=1.6, in1=st.pop(("z1", c))[:], op0=ALU.add, op1=ALU.mult
             )
@@ -454,7 +481,7 @@ def tile_chunkflooredmessagemiddlescore_kernel(
 
         def rC(c):
             if c % 2 == 0:
-                rg = work.tile([P, 2, P, 4], BF16, name="rg", tag="rg", bufs=2, align_bytes=64)
+                rg = work.tile([P, 2, P, 4], BF16, name="rg", tag="rg", bufs=3, align_bytes=64)
                 st["rg", c // 2] = rg
             eng = nc.vector.tensor_copy if c in VRC else nc.scalar.copy
             eng(out=st["rg", c // 2][:, c % 2, :, :], in_=st.pop(("rt", c))[:].rearrange("p j r -> p r j"))
@@ -474,13 +501,14 @@ def tile_chunkflooredmessagemiddlescore_kernel(
 
         v0 = lambda f: (lambda c: f(c, 0))
         v1 = lambda f: (lambda c: f(c, 1))
+        v3 = lambda f, i: (lambda c: f(i))
         ops = {
-            "kB": kB, "kG": kG, "tI": tI, "tQ": tQ, "xT": xT, "xC": xC, "xQ": xQ, "eM": eM, "eS": eS, "eT": eT,
+            "kB0": v3(kB, 0), "kB1": v3(kB, 1), "kB2": v3(kB, 2), "kG0": v3(kG, 0), "kG1": v3(kG, 1), "tI": tI, "tQ": tQ, "xT": xT, "xC": xC, "xQ": xQ, "eM": eM, "eS": eS, "eT": eT,
             "eN": eN, "eX": eX, "eE": eE, "vR": vR, "vG0": v0(vG), "vG1": v1(vG), "vM0": v0(vM), "vM1": v1(vM),
             "vT": vT, "vC": vC, "vQ": vQ, "mM": mM, "f0": f0, "f1": f1, "zP": zP, "zE": zE, "zA": zA, "zR": zR,
             "rL": rL, "rA": rA, "rT": rT, "rC": rC, "rQ": rQ,
         }
-        count = {"u": len(units), "c": CHUNKS, "t": CHUNKS, "k": 3, "g": 2, "i": 2 * TPARTS, "q": 2}
+        count = {"u": len(units), "c": CHUNKS, "t": CHUNKS, "k": 1, "g": 2, "i": 2 * TPARTS, "q": 2}
         for s in range(60):
             for op, kind, lag in ORDER:
                 j = s - lag

@@ -21,11 +21,11 @@ G = D // 512
 FLOPS = 2 * LAYERS * TOKENS * D * T + 2 * 2 * TOKENS * T * T
 MANUAL = True
 LORD = (0, 2, 1)
-TR = ()
+TR = (1, 4, 7, 10, 13, 16, 19, 22, 0, 3, 6, 9, 12, 15, 18, 21)
 VG = ()
-EZG = (0, 1, 2, 3, 4, 5)
+EZG = ()
 VXC = ()
-VRC = (1, 3, 5, 7)
+VRC = (3, 7)
 GSPLIT = 1
 TE = "G"
 TPARTS = 2
@@ -36,45 +36,42 @@ MB = 2
 TB = 1
 VCE = "S"
 ORDER = [
-    ("mM", "c", 9),
-    ("vG0", "c", 5),
-    ("eN", "u", 2),
+    ("vQ", "c", 9),
     ("xQ", "u", 1),
-    ("zE", "c", 12),
-    ("kG1", "k", 3),
-    ("kG0", "k", 2),
-    ("zA", "c", 13),
-    ("f0", "c", 10),
-    ("vM1", "c", 6),
-    ("zR", "c", 13),
-    ("vG1", "c", 10),
-    ("vQ", "c", 8),
-    ("vT", "c", 7),
-    ("eE", "u", 3),
-    ("tQ", "q", 6),
-    ("eX", "u", 2),
-    ("vR", "c", 4),
-    ("rC", "t", 31),
-    ("kB0", "k", 1),
-    ("kB2", "k", 2),
-    ("rA", "t", 28),
-    ("vM0", "c", 5),
-    ("kB1", "k", 1),
-    ("tI", "i", 3),
+    ("kG0", "k", 3),
+    ("f0", "c", 11),
+    ("rT", "t", 31),
+    ("tI", "i", 6),
+    ("mM", "c", 10),
+    ("tQ", "q", 8),
+    ("vT", "c", 8),
     ("xT", "u", 0),
+    ("kB0", "k", 1),
+    ("f1", "c", 11),
+    ("zR", "c", 14),
+    ("eX", "u", 3),
+    ("eS", "u", 2),
+    ("rA", "t", 29),
+    ("eE", "u", 4),
     ("eM", "u", 1),
-    ("vC", "c", 7),
-    ("rL", "t", 27),
+    ("vM0", "c", 7),
+    ("zP", "c", 11),
     ("rQ", "t", 34),
-    ("zP", "c", 10),
-    ("f1", "c", 9),
-    ("rT", "t", 30),
+    ("vM1", "c", 7),
+    ("vR", "c", 5),
+    ("vC", "c", 8),
+    ("zE", "c", 12),
+    ("eT", "u", 2),
+    ("kG1", "k", 2),
+    ("rC", "t", 31),
+    ("rL", "t", 28),
+    ("eN", "u", 1),
     ("xC", "u", 0),
 ]
 DUM = 0
 ZG = ()
-W = (0, 1, 2, 3, 4, 5, 6)
-KBV = (0, 1, 2)
+W = ()
+TSPL = 4
 
 
 def tile_chunkflooredmessagemiddlescore_kernel(
@@ -97,14 +94,13 @@ def tile_chunkflooredmessagemiddlescore_kernel(
 
         we = keep.tile([P, G, 2 * T], U8, name="we", align_bytes=64)
         wscale = keep.tile([P, G, T], U8, name="wscale", align_bytes=64)
-        rows = keep.tile([P, 5, T], BF16, name="rows", align_bytes=64)
+        rows = keep.tile([P, 3, T], BF16, name="rows", align_bytes=64)
         ones = keep.tile([P, P], BF16, name="ones", align_bytes=64)
         ident = keep.tile([P, P], F32, name="ident")
         make_identity(nc, ident[:])
         nc.vector.memset(rows[:, 0:3, :], 0.0)
         nc.vector.memset(wscale[:].rearrange("p g n -> p (g n)").bitcast(I32), 0)
         nc.vector.memset(ones[:], 1.0)
-        nc.vector.memset(rows[:, 3:5, :], 0.0)
         load_x(0, LORD[0])
         nc.sync.dma_start(
             out=we[:].rearrange("p g n -> p (g n)").bitcast(I32).rearrange("p (g n) -> p g n", g=G),
@@ -117,11 +113,12 @@ def tile_chunkflooredmessagemiddlescore_kernel(
             )
         nc.scalar.dma_start(out=rows[0:1, 0:3, :], in_=be.unsqueeze(0).unsqueeze(0).to_broadcast([1, 3, T]))
         nc.scalar.dma_start(out=rows[1:2, 0:2, :], in_=ends.unsqueeze(0))
-        nc.scalar.dma_start(out=rows[0:1, 3:5, :], in_=gain.unsqueeze(0))
         load_x(0, LORD[1])
         load_x(0, LORD[2])
         for layer in LORD:
             load_x(1, layer)
+        graw = keep.tile([P, 2 * T], BF16, name="graw", align_bytes=64)
+        nc.sync.dma_start(out=graw[:], in_=gain.rearrange("p t -> (p t)").partition_broadcast(P))
         traw = []
         for p in range(2):
             t = keep.tile([P, 4, T], BF16, name=f"traw_{p}", align_bytes=64)
@@ -143,21 +140,9 @@ def tile_chunkflooredmessagemiddlescore_kernel(
         BROW = {0: 0, 2: 1, 1: 2}
         bias, bcol, gain512 = {}, {}, {}
 
-        def kB(i):
-            layer = LORD[i]
-            row = BROW[layer]
-            acc = psum.tile([P, T], F32, name="acc", tag="e", bufs=EB)
-            nc.tensor.matmul(acc[:], lhsT=ones[:], rhs=rows[:, row, :], start=True, stop=True)
-            b = keep.tile([P, T], F32, name=f"bias_{layer}")
-            eng = nc.vector.tensor_copy if i in KBV else nc.scalar.copy
-            eng(out=b[:], in_=acc[:])
-            bias[layer] = b
-
         def kG(p):
-            acc = psum.tile([P, T], F32, name="acc", tag="m", bufs=MB)
-            nc.tensor.matmul(acc[:], lhsT=ones[:], rhs=rows[:, 3 + p, :], start=True, stop=True)
             g = keep.tile([P, T], F32, name=f"gain_{p}")
-            nc.scalar.activation(out=g[:], in_=acc[:], func=ACT.Copy, scale=512.0)
+            nc.scalar.activation(out=g[:], in_=graw[:, p * T : (p + 1) * T], func=ACT.Copy, scale=512.0)
             gain512[p] = g
 
         tcodes = keep.tile([P, 2, T], U32, name="tcodes", align_bytes=64)
@@ -168,17 +153,18 @@ def tile_chunkflooredmessagemiddlescore_kernel(
             tgrp.append(t)
 
         def tI(i):
-            p, part = divmod(i, TPARTS)
-            n = slice(part * T // TPARTS, (part + 1) * T // TPARTS)
-            src = traw[p][:, :, n].rearrange("k j n -> k n j")
-            if TE == "G":
-                nc.gpsimd.tensor_scalar(
-                    out=tgrp[p][:, n, :], in0=src, scalar1=1.0, scalar2=1.0, op0=ALU.mult, op1=ALU.mult
-                )
-            elif TE == "V":
-                nc.vector.tensor_copy(out=tgrp[p][:, n, :], in_=src)
-            else:
-                nc.scalar.copy(out=tgrp[p][:, n, :], in_=src)
+            for h in range(TSPL):
+                p, part = divmod(i * TSPL + h, 2 * TSPL)
+                n = slice(part * T // (2 * TSPL), (part + 1) * T // (2 * TSPL))
+                src = traw[p][:, :, n].rearrange("k j n -> k n j")
+                if TE == "G":
+                    nc.gpsimd.tensor_scalar(
+                        out=tgrp[p][:, n, :], in0=src, scalar1=1.0, scalar2=1.0, op0=ALU.mult, op1=ALU.mult
+                    )
+                elif TE == "V":
+                    nc.vector.tensor_copy(out=tgrp[p][:, n, :], in_=src)
+                else:
+                    nc.scalar.copy(out=tgrp[p][:, n, :], in_=src)
 
         def tQ(p):
             nc.vector.quantize_mx(
@@ -228,9 +214,8 @@ def tile_chunkflooredmessagemiddlescore_kernel(
         def eM(s):
             u = units[s]
             xq, xsc = st.pop(("xq", u))
-            if u[1] in TR:
+            if (3 * u[0] + u[1]) in TR:
                 acc = psum.tile([P, 4, P], F32, name="et", tag="et", bufs=TB)
-                warm_pass(acc[:].rearrange("p j n -> p (j n)"), xq, xsc)
                 for j in range(4):
                     for g in range(G):
                         nc.tensor.matmul_mx(
@@ -243,7 +228,6 @@ def tile_chunkflooredmessagemiddlescore_kernel(
                 st["et", u] = acc
             else:
                 acc = psum.tile([P, T], F32, name="e", tag="e", bufs=EB)
-                warm_pass(acc, xq, xsc)
                 for g in range(G):
                     nc.tensor.matmul_mx(
                         out=acc[:],
@@ -255,52 +239,57 @@ def tile_chunkflooredmessagemiddlescore_kernel(
 
         def eS(s):
             u = units[s]
-            if u[1] not in TR:
+            if (3 * u[0] + u[1]) not in TR:
                 return
             et = st.pop(("et", u))
             es = work.tile([P, 4, P], F32, name="es", tag="es", bufs=2)
-            for j in range(4):
-                nc.scalar.activation(out=es[:, j, :], in_=et[:, j, :], func=ACT.Identity, bias=bcol[u[1]][:, 2 * j : 2 * j + 1], scale=1.0)
+            nc.scalar.copy(out=es[:], in_=et[:])
             st["es", u] = es
 
         def eT(s):
             u = units[s]
-            if u[1] not in TR:
+            if (3 * u[0] + u[1]) not in TR:
                 return
             es = st.pop(("es", u))
             acc = psum.tile([P, T], F32, name="e", tag="e", bufs=EB)
+            nc.tensor.matmul(acc[:], lhsT=ones[:], rhs=rows[:, BROW[u[1]], :], start=True, stop=False)
             for j in range(4):
-                nc.tensor.transpose(acc[:, P * j : P * (j + 1)], es[:, j, :], ident[:])
+                nc.tensor.matmul(
+                    acc[:, P * j : P * (j + 1)], lhsT=es[:, j, :], rhs=ident[:], start=False, stop=j == 3, is_transpose=True
+                )
             st["e", u] = acc
+
+        def kB(layer):
+            acc = psum.tile([P, T], F32, name="acc", tag="e", bufs=EB)
+            nc.tensor.matmul(acc[:], lhsT=ones[:], rhs=rows[:, BROW[layer], :], start=True, stop=True)
+            b = keep.tile([P, T], F32, name=f"bias_{layer}")
+            nc.vector.tensor_copy(out=b[:], in_=acc[:])
+            bias[layer] = b
 
         def eN(s):
             u = units[s]
-            c, layer = u
-            if layer in TR:
+            if (3 * u[0] + u[1]) in TR:
                 return
-            if layer == 1:
-                n = keep.tile([P, T], F32, name=f"e1_{c}")
-            else:
-                n = work.tile([P, T], F32, name="n", tag="n", bufs=3)
-            nc.vector.tensor_tensor(out=n[:], in0=st.pop(("e", u))[:], in1=bias[layer][:], op=ALU.add)
-            st["n", u] = n
+            n = work.tile([P, T], F32, name="n", tag="n", bufs=3)
+            nc.vector.tensor_tensor(out=n[:], in0=st.pop(("e", u))[:], in1=bias[u[1]][:], op=ALU.add)
+            st["nn", u] = n
 
         def eX(s):
-            c, layer = units[s]
             u = units[s]
-            if layer in TR and layer == 1:
+            c, layer = u
+            e = st.pop(("e", u)) if (3 * c + layer) in TR else st.pop(("nn", u))
+            if layer == 1:
                 n = keep.tile([P, T], F32, name=f"e1_{c}")
                 nc.vector.tensor_scalar(
-                    out=n[:], in0=st.pop(("e", u))[:], scalar1=-1.0, scalar2=None, op0=ALU.mult, op1=ALU.min,
+                    out=n[:], in0=e[:], scalar1=-1.0, scalar2=None, op0=ALU.mult, op1=ALU.min,
                     accum_out=stats[c][:, 1:2],
                 )
                 st["n", u] = n
-                return
-            if layer in TR:
-                st["n", u] = st.pop(("e", u))
-            nc.vector.tensor_reduce(
-                out=stats[c][:, layer : layer + 1], in_=st["n", u][:], axis=AX.X, op=ALU.max, negate=True
-            )
+            else:
+                nc.vector.tensor_reduce(
+                    out=stats[c][:, layer : layer + 1], in_=e[:], axis=AX.X, op=ALU.max, negate=True
+                )
+                st["n", u] = e
 
         def eE(s):
             u = units[s]
@@ -309,7 +298,7 @@ def tile_chunkflooredmessagemiddlescore_kernel(
             n = st["n", u]
             if layer == 1:
                 nc.scalar.activation(
-                    out=ex[:], in_=n[:], func=ACT.Exp, bias=stats[c][:, 1:2], scale=-1.0 if 1 in TR else 1.0
+                    out=ex[:], in_=n[:], func=ACT.Exp, bias=stats[c][:, 1:2], scale=-1.0 if True else 1.0
                 )
             else:
                 st.pop(("n", u))
@@ -347,7 +336,7 @@ def tile_chunkflooredmessagemiddlescore_kernel(
             st["v", c, p] = v
 
         def vT(c):
-            vt = psum.tile([P, 2, 2, P], F32, name="vt", tag="vt", bufs=VB)
+            vt = psum.tile([P, 2, 2, P], F32, name="vt", tag="xt", bufs=XB)
             for p in range(2):
                 w = st.pop(("v", c, p))[:].bitcast(F32)
                 for h in range(2):
@@ -461,7 +450,7 @@ def tile_chunkflooredmessagemiddlescore_kernel(
         def rA(c):
             r = work.tile([P, T], F32, name="r", tag="r", bufs=4)
             n, lz = st.pop(("n", (c, 1))), st.pop(("lz", c))
-            if 1 in TR:
+            if True:
                 nc.vector.scalar_tensor_tensor(
                     out=r[:], in0=lz[:], scalar=stats[c][:, 1:2], in1=n[:], op0=ALU.add, op1=ALU.subtract
                 )
@@ -503,12 +492,12 @@ def tile_chunkflooredmessagemiddlescore_kernel(
         v1 = lambda f: (lambda c: f(c, 1))
         v3 = lambda f, i: (lambda c: f(i))
         ops = {
-            "kB0": v3(kB, 0), "kB1": v3(kB, 1), "kB2": v3(kB, 2), "kG0": v3(kG, 0), "kG1": v3(kG, 1), "tI": tI, "tQ": tQ, "xT": xT, "xC": xC, "xQ": xQ, "eM": eM, "eS": eS, "eT": eT,
-            "eN": eN, "eX": eX, "eE": eE, "vR": vR, "vG0": v0(vG), "vG1": v1(vG), "vM0": v0(vM), "vM1": v1(vM),
+            "eN": eN, "kB0": v3(kB, 2), "kB1": v3(kB, 0), "kG0": v3(kG, 0), "kG1": v3(kG, 1), "tI": tI, "tQ": tQ, "xT": xT, "xC": xC, "xQ": xQ, "eM": eM, "eS": eS, "eT": eT,
+            "eX": eX, "eE": eE, "vR": vR, "vG0": v0(vG), "vG1": v1(vG), "vM0": v0(vM), "vM1": v1(vM),
             "vT": vT, "vC": vC, "vQ": vQ, "mM": mM, "f0": f0, "f1": f1, "zP": zP, "zE": zE, "zA": zA, "zR": zR,
             "rL": rL, "rA": rA, "rT": rT, "rC": rC, "rQ": rQ,
         }
-        count = {"u": len(units), "c": CHUNKS, "t": CHUNKS, "k": 1, "g": 2, "i": 2 * TPARTS, "q": 2}
+        count = {"u": len(units), "c": CHUNKS, "t": CHUNKS, "k": 1, "g": 2, "i": 4, "q": 2}
         for s in range(60):
             for op, kind, lag in ORDER:
                 j = s - lag

@@ -12,66 +12,69 @@ FP8X4 = mybir.dt.float8_e4m3fn_x4
 FP4X4 = mybir.dt.float4_e2m1fn_x4
 ALU = mybir.AluOpType
 ACT = mybir.ActivationFunctionType
-AX = mybir.AxisListType
+AXIS = mybir.AxisListType
 
-LAYERS, TOKENS, D, T = 3, 1024, 1024, 512
-P = 128
-CHUNKS = TOKENS // P
-G = D // 512
-FLOPS = 2 * LAYERS * TOKENS * D * T + 2 * 2 * TOKENS * T * T
-MANUAL = True
-LORD = (0, 2, 1)
-TR = (1, 4, 7, 10, 13, 16, 19, 22, 0, 3, 6, 9, 12, 15, 18, 21)
-VG = ()
-EZG = ()
-VXC = ()
-VRC = (3, 7)
-GSPLIT = 1
-TE = "G"
-TPARTS = 2
-EB = 3
-XB = 2
-VB = 1
-MB = 2
-TB = 1
-VCE = "S"
-ORDER = [
-    ("vQ", "c", 9),
-    ("xQ", "u", 1),
-    ("kG0", "k", 3),
-    ("f0", "c", 11),
-    ("rT", "t", 31),
-    ("tI", "i", 6),
-    ("mM", "c", 10),
-    ("tQ", "q", 8),
-    ("vT", "c", 8),
-    ("xT", "u", 0),
-    ("kB0", "k", 1),
-    ("f1", "c", 11),
-    ("zR", "c", 14),
-    ("eX", "u", 3),
-    ("eS", "u", 2),
-    ("rA", "t", 29),
-    ("eE", "u", 4),
-    ("eM", "u", 1),
-    ("vM0", "c", 7),
-    ("zP", "c", 11),
-    ("rQ", "t", 34),
-    ("vM1", "c", 7),
-    ("vR", "c", 5),
-    ("vC", "c", 8),
-    ("zE", "c", 12),
-    ("eT", "u", 2),
-    ("kG1", "k", 2),
-    ("rC", "t", 31),
-    ("rL", "t", 28),
-    ("eN", "u", 1),
-    ("xC", "u", 0),
-]
-DUM = 0
-ZG = ()
-W = ()
-TSPL = 4
+LAYERS, TOKENS, D, TAGS = 3, 1024, 1024, 512
+PART = 128
+CHUNKS = TOKENS // PART
+PASSES = D // 512
+PACK = 4
+QUARTERS = TAGS // PART
+FLOPS = 2 * LAYERS * TOKENS * D * TAGS + 2 * 2 * TOKENS * TAGS * TAGS
+
+FLOOR = 14.4
+ABOVE = 1.6
+
+LAYER_ORDER = (0, 2, 1)
+BIAS_ROW = {0: 0, 2: 1, 1: 2}
+TRANS_BEFORE = (2, 3)
+
+ISSUE_ORDER = (
+    ("pass_messages", "chunk", 10),
+    ("save_scores", "tile", 2),
+    ("quantise_trans_0", "once", 9),
+    ("quantise_trans_1", "once", 5),
+    ("quantise_x", "tile", 1),
+    ("add_bias", "tile", 2),
+    ("interleave_trans_1b", "once", 4),
+    ("spread_bias_0", "once", 1),
+    ("spread_gain_1", "once", 1),
+    ("take_log", "tail", 28),
+    ("floor_second", "chunk", 11),
+    ("exponentiate", "tile", 4),
+    ("copy_result", "tail", 31),
+    ("turn_x", "tile", 0),
+    ("quantise_messages", "chunk", 9),
+    ("interleave_trans_0b", "once", 2),
+    ("find_maximum", "tile", 3),
+    ("spread_bias_2", "once", 0),
+    ("invert_total", "chunk", 13),
+    ("copy_x", "tile", 0),
+    ("turn_messages", "chunk", 8),
+    ("weigh_first", "chunk", 7),
+    ("turn_result", "tail", 30),
+    ("interleave_trans_1a", "once", 2),
+    ("multiply_x", "tile", 1),
+    ("invert_sums", "chunk", 6),
+    ("sum_weighted", "chunk", 12),
+    ("weigh_second", "chunk", 7),
+    ("copy_messages", "chunk", 8),
+    ("return_scores", "tile", 2),
+    ("quantise_result", "tail", 35),
+    ("spread_gain_0", "once", 2),
+    ("finish_result", "tail", 29),
+    ("multiply_floors", "chunk", 11),
+    ("floor_first", "chunk", 10),
+    ("interleave_trans_0a", "once", 4),
+)
+
+
+TENSOR_BIAS_CHUNKS = (2, 4, 6)
+SCALAR_FLOOR_CHUNKS = (2, 4)
+
+
+def bias_on_tensor(chunk, layer):
+    return layer == 1 or (layer == 0 and chunk in TENSOR_BIAS_CHUNKS)
 
 
 def tile_chunkflooredmessagemiddlescore_kernel(
@@ -82,433 +85,428 @@ def tile_chunkflooredmessagemiddlescore_kernel(
         keep = ctx.enter_context(tc.tile_pool(name="keep", bufs=1))
         work = ctx.enter_context(tc.tile_pool(name="work", bufs=3))
         psum = ctx.enter_context(tc.psum_pool(name="psum", bufs=2))
-        if MANUAL:
-            ctx.enter_context(tc.manual_schedule())
+        ctx.enter_context(tc.manual_schedule())
 
-        xs = {}
-
-        def load_x(c, layer):
-            t = keep.tile([P, D], BF16, name=f"x_{c}_{layer}", align_bytes=64)
-            nc.sync.dma_start(out=t[:], in_=x[layer, c * P : (c + 1) * P, :])
-            xs[c, layer] = t
-
-        we = keep.tile([P, G, 2 * T], U8, name="we", align_bytes=64)
-        wscale = keep.tile([P, G, T], U8, name="wscale", align_bytes=64)
-        rows = keep.tile([P, 3, T], BF16, name="rows", align_bytes=64)
-        ones = keep.tile([P, P], BF16, name="ones", align_bytes=64)
-        ident = keep.tile([P, P], F32, name="ident")
+        x_tiles = {}
+        words = keep.tile([PART, PASSES, 2 * TAGS], U8, name="we_words", align_bytes=64)
+        word_scales = keep.tile([PART, PASSES, TAGS], U8, name="we_scales", align_bytes=64)
+        rows = keep.tile([PART, 5, TAGS], BF16, name="rows", align_bytes=64)
+        ones = keep.tile([PART, PART], BF16, name="ones", align_bytes=64)
+        ident = keep.tile([PART, PART], F32, name="ident")
         make_identity(nc, ident[:])
         nc.vector.memset(rows[:, 0:3, :], 0.0)
-        nc.vector.memset(wscale[:].rearrange("p g n -> p (g n)").bitcast(I32), 0)
-        nc.vector.memset(ones[:], 1.0)
-        load_x(0, LORD[0])
-        nc.sync.dma_start(
-            out=we[:].rearrange("p g n -> p (g n)").bitcast(I32).rearrange("p (g n) -> p g n", g=G),
-            in_=we_words.bitcast(I32).rearrange("g p n -> p g n"),
-        )
-        for q in range(4):
+        nc.vector.memset(word_scales[:].rearrange("p g n -> p (g n)").bitcast(I32), 0)
+        nc.vector.memset(ones[:], 0.0)
+        nc.vector.memset(rows[:, 3:5, :], 0.0)
+
+        def load_x(chunk, layer):
+            tile = keep.tile([PART, D], BF16, name=f"x_{chunk}_{layer}", align_bytes=64)
+            nc.sync.dma_start(out=tile[:], in_=x[layer, chunk * PART : (chunk + 1) * PART, :])
+            x_tiles[chunk, layer] = tile
+
+        def as_words(ap):
+            return ap.rearrange("p g n -> p (g n)").bitcast(I32).rearrange("p (g n) -> p g n", g=PASSES)
+
+        tiles = [(chunk, layer) for chunk in range(CHUNKS) for layer in LAYER_ORDER]
+        load_x(*tiles[0])
+        nc.sync.dma_start(out=as_words(words[:]), in_=we_words.bitcast(I32).rearrange("g p n -> p g n"))
+        for quadrant in range(4):
             nc.sync.dma_start(
-                out=wscale[32 * q : 32 * q + 4, :, :].rearrange("p g n -> p (g n)").bitcast(I32).rearrange("p (g n) -> p g n", g=G),
-                in_=we_scales[:, 4 * q : 4 * q + 4, :].bitcast(I32).rearrange("g r n -> r g n"),
+                out=as_words(word_scales[32 * quadrant : 32 * quadrant + 4, :, :]),
+                in_=we_scales[:, 4 * quadrant : 4 * quadrant + 4, :].bitcast(I32).rearrange("g r n -> r g n"),
             )
-        nc.scalar.dma_start(out=rows[0:1, 0:3, :], in_=be.unsqueeze(0).unsqueeze(0).to_broadcast([1, 3, T]))
+        nc.scalar.dma_start(
+            out=rows[0:1, 0:3, :], in_=be.unsqueeze(0).unsqueeze(0).to_broadcast([1, 3, TAGS])
+        )
         nc.scalar.dma_start(out=rows[1:2, 0:2, :], in_=ends.unsqueeze(0))
-        load_x(0, LORD[1])
-        load_x(0, LORD[2])
-        for layer in LORD:
-            load_x(1, layer)
-        graw = keep.tile([P, 2 * T], BF16, name="graw", align_bytes=64)
-        nc.sync.dma_start(out=graw[:], in_=gain.rearrange("p t -> (p t)").partition_broadcast(P))
-        traw = []
+        nc.scalar.dma_start(out=rows[0:1, 3:5, :], in_=gain.unsqueeze(0))
+        trans_raw = {}
+        for place, tile_id in enumerate(tiles[1:]):
+            for p in range(2):
+                if place == TRANS_BEFORE[p]:
+                    raw = keep.tile([PART, PACK, TAGS], BF16, name=f"trans_raw_{p}", align_bytes=64)
+                    nc.sync.dma_start(out=raw[:], in_=trans[p].rearrange("(k j) n -> k j n", j=PACK))
+                    trans_raw[p] = raw
+            load_x(*tile_id)
+        nc.scalar.activation(out=ones[:], in_=ones[:], func=ACT.Exp)
+
+        trans_codes = keep.tile([PART, 2, TAGS], U32, name="trans_codes", align_bytes=64)
+        trans_scales = keep.tile([PART, 2, TAGS], U8, name="trans_scales", align_bytes=64)
+        trans_grouped = []
         for p in range(2):
-            t = keep.tile([P, 4, T], BF16, name=f"traw_{p}", align_bytes=64)
-            nc.sync.dma_start(out=t[:], in_=trans[p].rearrange("(k j) n -> k j n", j=4))
-            traw.append(t)
-        for c in range(2, CHUNKS):
-            for layer in LORD:
-                load_x(c, layer)
-        warm = keep.tile([P, 1], F32, name="warm")
-        nc.vector.memset(warm[:], 0.0)
-        nc.scalar.activation(out=warm[:], in_=warm[:], func=ACT.Exp)
+            grouped = keep.tile([PART, TAGS, PACK], BF16, name=f"trans_grouped_{p}", align_bytes=64)
+            trans_grouped.append(grouped)
+        stats = []
+        for chunk in range(CHUNKS):
+            columns = keep.tile([PART, 16], F32, name=f"stats_{chunk}")
+            stats.append(columns)
+        result_codes = keep.tile([PART, TOKENS], U32, name="result_codes", align_bytes=64)
+        result_scales = keep.tile([PART, TOKENS], U8, name="result_scales", align_bytes=64)
+        bias = {}
+        gain512 = {}
+        live = {}
 
-        st = {}
-        stats = {}
-        for c in range(CHUNKS):
-            s = keep.tile([P, 16], F32, name=f"stats_{c}")
-            stats[c] = s
-        units = [(c, layer) for c in range(CHUNKS) for layer in LORD]
-        BROW = {0: 0, 2: 1, 1: 2}
-        bias, bcol, gain512 = {}, {}, {}
+        def spread(block, tag, bufs):
+            acc = psum.tile([PART, TAGS], F32, name="spread", tag=tag, bufs=bufs)
+            nc.tensor.matmul(acc[:], lhsT=ones[:], rhs=rows[:, block, :], start=True, stop=True)
+            return acc
 
-        def kG(p):
-            g = keep.tile([P, T], F32, name=f"gain_{p}")
-            nc.scalar.activation(out=g[:], in_=graw[:, p * T : (p + 1) * T], func=ACT.Copy, scale=512.0)
-            gain512[p] = g
+        def spread_bias(layer):
+            acc = spread(BIAS_ROW[layer], "scores", 3)
+            full = keep.tile([PART, TAGS], F32, name=f"bias_{layer}")
+            nc.vector.tensor_copy(out=full[:], in_=acc[:])
+            bias[layer] = full
 
-        tcodes = keep.tile([P, 2, T], U32, name="tcodes", align_bytes=64)
-        tscale = keep.tile([P, 2, T], U8, name="tscale", align_bytes=64)
-        tgrp = []
-        for p in range(2):
-            t = keep.tile([P, T, 4], BF16, name=f"tgrp_{p}", align_bytes=64)
-            tgrp.append(t)
+        def spread_gain(p):
+            acc = spread(3 + p, "passed", 2)
+            full = keep.tile([PART, TAGS], F32, name=f"gain512_{p}")
+            nc.scalar.activation(out=full[:], in_=acc[:], func=ACT.Copy, scale=512.0)
+            gain512[p] = full
 
-        def tI(i):
-            for h in range(TSPL):
-                p, part = divmod(i * TSPL + h, 2 * TSPL)
-                n = slice(part * T // (2 * TSPL), (part + 1) * T // (2 * TSPL))
-                src = traw[p][:, :, n].rearrange("k j n -> k n j")
-                if TE == "G":
-                    nc.gpsimd.tensor_scalar(
-                        out=tgrp[p][:, n, :], in0=src, scalar1=1.0, scalar2=1.0, op0=ALU.mult, op1=ALU.mult
-                    )
-                elif TE == "V":
-                    nc.vector.tensor_copy(out=tgrp[p][:, n, :], in_=src)
-                else:
-                    nc.scalar.copy(out=tgrp[p][:, n, :], in_=src)
-
-        def tQ(p):
-            nc.vector.quantize_mx(
-                out=tcodes[:, p, :].bitcast(FP8X4), scales=tscale[:, p, :],
-                in_=tgrp[p][:].rearrange("k n j -> k (n j)"),
+        def interleave_trans(p, half):
+            cols = slice(half * TAGS // 2, (half + 1) * TAGS // 2)
+            nc.vector.tensor_copy(
+                out=trans_grouped[p][:, cols, :], in_=trans_raw[p][:, :, cols].rearrange("k j n -> k n j")
             )
 
-        def xT(s):
-            u = units[s]
-            xt = psum.tile([P, G, 2, P], F32, name="xt", tag="xt", bufs=XB)
-            w = xs[u][:].bitcast(F32)
-            for g in range(G):
+        def quantise_trans(p):
+            nc.vector.quantize_mx(
+                out=trans_codes[:, p, :].bitcast(FP8X4),
+                scales=trans_scales[:, p, :],
+                in_=trans_grouped[p][:].rearrange("k n j -> k (n j)"),
+            )
+
+        def turn_x(tile):
+            turned = psum.tile([PART, PASSES, 2, PART], F32, name="x_turned", tag="turned", bufs=2)
+            pairs = x_tiles[tiles[tile]][:].bitcast(F32)
+            for g in range(PASSES):
                 for h in range(2):
-                    nc.tensor.transpose(xt[:, g, h, :], w[:, 256 * g + h : 256 * (g + 1) : 2], ident[:])
-            st["xt", u] = xt
+                    nc.tensor.transpose(turned[:, g, h, :], pairs[:, 256 * g + h : 256 * (g + 1) : 2], ident[:])
+            live["x_turned", tile] = turned
 
-        def xC(s):
-            u = units[s]
-            xg = work.tile([P, G * P * 4], BF16, name="xg", tag="xg", bufs=3, align_bytes=64)
-            eng = nc.vector.tensor_copy if s in VXC else nc.scalar.copy
-            eng(
-                out=xg[:].bitcast(F32).rearrange("p (g r h) -> p g r h", g=G, h=2),
-                in_=st.pop(("xt", u))[:].rearrange("p g h r -> p g r h"),
+        def copy_x(tile):
+            grouped = work.tile([PART, PASSES * PART * PACK], BF16, name="x_grouped", bufs=3, align_bytes=64)
+            nc.scalar.copy(
+                out=grouped[:].bitcast(F32).rearrange("p (g r h) -> p g r h", g=PASSES, h=2),
+                in_=live.pop(("x_turned", tile))[:].rearrange("p g h r -> p g r h"),
             )
-            st["xg", u] = xg
+            live["x_grouped", tile] = grouped
 
-        def xQ(s):
-            u = units[s]
-            xq = work.tile([P, G, P], U32, name="xq", tag="xq", bufs=3, align_bytes=64)
-            xsc = work.tile([P, G, P], U8, name="xsc", tag="xsc", bufs=3, align_bytes=64)
+        def quantise_x(tile):
+            codes = work.tile([PART, PASSES, PART], U32, name="x_codes", bufs=3, align_bytes=64)
+            scales = work.tile([PART, PASSES, PART], U8, name="x_scales", bufs=3, align_bytes=64)
             nc.vector.quantize_mx(
-                out=xq[:].rearrange("p g r -> p (g r)").bitcast(FP8X4),
-                scales=xsc[:].rearrange("p g r -> p (g r)"),
-                in_=st.pop(("xg", u))[:],
+                out=codes[:].rearrange("p g r -> p (g r)").bitcast(FP8X4),
+                scales=scales[:].rearrange("p g r -> p (g r)"),
+                in_=live.pop(("x_grouped", tile))[:],
             )
-            st["xq", u] = (xq, xsc)
+            live["x_codes", tile] = (codes, scales)
 
-        def warm_pass(acc, xq, xsc):
-            for g in range(DUM):
-                nc.tensor.matmul_mx(
-                    out=acc[:],
-                    lhsT=xq[:, g, :].bitcast(FP8X4), lhsT_scale=xsc[:, g, :],
-                    rhs=we[:, g, :].bitcast(FP4X4), rhs_scale=wscale[:, g, :],
-                    start=True, stop=True,
-                )
-
-        def eM(s):
-            u = units[s]
-            xq, xsc = st.pop(("xq", u))
-            if (3 * u[0] + u[1]) in TR:
-                acc = psum.tile([P, 4, P], F32, name="et", tag="et", bufs=TB)
-                for j in range(4):
-                    for g in range(G):
+        def multiply_x(tile):
+            codes, scales = live.pop(("x_codes", tile))
+            if bias_on_tensor(*tiles[tile]):
+                acc = psum.tile([PART, QUARTERS, PART], F32, name="flipped", tag="flipped", bufs=1)
+                for q in range(QUARTERS):
+                    for g in range(PASSES):
                         nc.tensor.matmul_mx(
-                            out=acc[:, j, :],
-                            lhsT=we[:, g, 2 * P * j : 2 * P * (j + 1)].bitcast(FP4X4),
-                            lhsT_scale=wscale[:, g, P * j : P * (j + 1)],
-                            rhs=xq[:, g, :].bitcast(FP8X4), rhs_scale=xsc[:, g, :],
-                            start=g == 0, stop=g == G - 1,
+                            out=acc[:, q, :],
+                            lhsT=words[:, g, 2 * PART * q : 2 * PART * (q + 1)].bitcast(FP4X4),
+                            lhsT_scale=word_scales[:, g, PART * q : PART * (q + 1)],
+                            rhs=codes[:, g, :].bitcast(FP8X4),
+                            rhs_scale=scales[:, g, :],
+                            start=g == 0,
+                            stop=g == PASSES - 1,
                         )
-                st["et", u] = acc
             else:
-                acc = psum.tile([P, T], F32, name="e", tag="e", bufs=EB)
-                for g in range(G):
+                acc = psum.tile([PART, TAGS], F32, name="scores", tag="scores", bufs=3)
+                for g in range(PASSES):
                     nc.tensor.matmul_mx(
                         out=acc[:],
-                        lhsT=xq[:, g, :].bitcast(FP8X4), lhsT_scale=xsc[:, g, :],
-                        rhs=we[:, g, :].bitcast(FP4X4), rhs_scale=wscale[:, g, :],
-                        start=g == 0, stop=g == G - 1,
+                        lhsT=codes[:, g, :].bitcast(FP8X4),
+                        lhsT_scale=scales[:, g, :],
+                        rhs=words[:, g, :].bitcast(FP4X4),
+                        rhs_scale=word_scales[:, g, :],
+                        start=g == 0,
+                        stop=g == PASSES - 1,
                     )
-                st["e", u] = acc
+            live["product", tile] = acc
 
-        def eS(s):
-            u = units[s]
-            if (3 * u[0] + u[1]) not in TR:
+        def save_scores(tile):
+            if not bias_on_tensor(*tiles[tile]):
                 return
-            et = st.pop(("et", u))
-            es = work.tile([P, 4, P], F32, name="es", tag="es", bufs=2)
-            nc.scalar.copy(out=es[:], in_=et[:])
-            st["es", u] = es
+            saved = work.tile([PART, QUARTERS, PART], F32, name="saved", bufs=2)
+            nc.scalar.copy(out=saved[:], in_=live.pop(("product", tile))[:])
+            live["saved", tile] = saved
 
-        def eT(s):
-            u = units[s]
-            if (3 * u[0] + u[1]) not in TR:
+        def return_scores(tile):
+            if not bias_on_tensor(*tiles[tile]):
                 return
-            es = st.pop(("es", u))
-            acc = psum.tile([P, T], F32, name="e", tag="e", bufs=EB)
-            nc.tensor.matmul(acc[:], lhsT=ones[:], rhs=rows[:, BROW[u[1]], :], start=True, stop=False)
-            for j in range(4):
+            saved = live.pop(("saved", tile))
+            acc = psum.tile([PART, TAGS], F32, name="scores", tag="scores", bufs=3)
+            block = BIAS_ROW[tiles[tile][1]]
+            nc.tensor.matmul(acc[:], lhsT=ones[:], rhs=rows[:, block, :], start=True, stop=False)
+            for q in range(QUARTERS):
                 nc.tensor.matmul(
-                    acc[:, P * j : P * (j + 1)], lhsT=es[:, j, :], rhs=ident[:], start=False, stop=j == 3, is_transpose=True
+                    acc[:, PART * q : PART * (q + 1)],
+                    lhsT=saved[:, q, :],
+                    rhs=ident[:],
+                    start=False,
+                    stop=q == QUARTERS - 1,
+                    is_transpose=True,
                 )
-            st["e", u] = acc
+            live["biased", tile] = acc
 
-        def kB(layer):
-            acc = psum.tile([P, T], F32, name="acc", tag="e", bufs=EB)
-            nc.tensor.matmul(acc[:], lhsT=ones[:], rhs=rows[:, BROW[layer], :], start=True, stop=True)
-            b = keep.tile([P, T], F32, name=f"bias_{layer}")
-            nc.vector.tensor_copy(out=b[:], in_=acc[:])
-            bias[layer] = b
-
-        def eN(s):
-            u = units[s]
-            if (3 * u[0] + u[1]) in TR:
+        def add_bias(tile):
+            if bias_on_tensor(*tiles[tile]):
                 return
-            n = work.tile([P, T], F32, name="n", tag="n", bufs=3)
-            nc.vector.tensor_tensor(out=n[:], in0=st.pop(("e", u))[:], in1=bias[u[1]][:], op=ALU.add)
-            st["nn", u] = n
+            biased = work.tile([PART, TAGS], F32, name="biased", bufs=3)
+            nc.vector.tensor_tensor(
+                out=biased[:], in0=live.pop(("product", tile))[:], in1=bias[tiles[tile][1]][:], op=ALU.add
+            )
+            live["biased", tile] = biased
 
-        def eX(s):
-            u = units[s]
-            c, layer = u
-            e = st.pop(("e", u)) if (3 * c + layer) in TR else st.pop(("nn", u))
+        def find_maximum(tile):
+            chunk, layer = tiles[tile]
+            biased = live.pop(("biased", tile))
+            column = stats[chunk][:, layer : layer + 1]
             if layer == 1:
-                n = keep.tile([P, T], F32, name=f"e1_{c}")
+                negated = keep.tile([PART, TAGS], F32, name=f"negated_{chunk}")
                 nc.vector.tensor_scalar(
-                    out=n[:], in0=e[:], scalar1=-1.0, scalar2=None, op0=ALU.mult, op1=ALU.min,
-                    accum_out=stats[c][:, 1:2],
+                    out=negated[:],
+                    in0=biased[:],
+                    scalar1=-1.0,
+                    scalar2=None,
+                    op0=ALU.mult,
+                    op1=ALU.min,
+                    accum_out=column,
                 )
-                st["n", u] = n
+                live["negated", chunk] = negated
             else:
-                nc.vector.tensor_reduce(
-                    out=stats[c][:, layer : layer + 1], in_=e[:], axis=AX.X, op=ALU.max, negate=True
-                )
-                st["n", u] = e
+                nc.vector.tensor_reduce(out=column, in_=biased[:], axis=AXIS.X, op=ALU.max, negate=True)
+                live["scores", tile] = biased
 
-        def eE(s):
-            u = units[s]
-            c, layer = u
-            ex = work.tile([P, T], F32, name="ex", tag=f"ex{layer}", bufs=3)
-            n = st["n", u]
+        def exponentiate(tile):
+            chunk, layer = tiles[tile]
+            column = stats[chunk][:, layer : layer + 1]
+            powers = work.tile([PART, TAGS], F32, name=f"powers_{layer}", bufs=3)
             if layer == 1:
                 nc.scalar.activation(
-                    out=ex[:], in_=n[:], func=ACT.Exp, bias=stats[c][:, 1:2], scale=-1.0 if True else 1.0
+                    out=powers[:], in_=live["negated", chunk][:], func=ACT.Exp, bias=column, scale=-1.0
                 )
             else:
-                st.pop(("n", u))
+                p = layer // 2
                 nc.scalar.activation(
-                    out=ex[:], in_=n[:], func=ACT.Exp, bias=stats[c][:, layer : layer + 1], scale=1.0,
-                    accum_out=stats[c][:, 4 + layer // 2 : 5 + layer // 2],
+                    out=powers[:],
+                    in_=live.pop(("scores", tile))[:],
+                    func=ACT.Exp,
+                    bias=column,
+                    scale=1.0,
+                    accum_out=stats[chunk][:, 4 + p : 5 + p],
                 )
-            st["ex", u] = ex
+            live["powers", chunk, layer] = powers
 
-        def vR(c):
-            s = stats[c]
-            nc.vector.reciprocal(out=s[:, 8:10], in_=s[:, 4:6])
+        def invert_sums(chunk):
+            nc.vector.reciprocal(out=stats[chunk][:, 8:10], in_=stats[chunk][:, 4:6])
 
-        def vG(c, p):
-            if 2 * c + p not in VG:
-                return
-            gx = work.tile([P, T], F32, name="gx", tag=f"gx{p}", bufs=2)
-            ex = st.pop(("ex", (c, 2 * p)))
-            for a in range(GSPLIT):
-                k = slice(a * T // GSPLIT, (a + 1) * T // GSPLIT)
-                nc.gpsimd.tensor_tensor(out=gx[:, k], in0=ex[:, k], in1=gain512[p][:, k], op=ALU.mult)
-            st["gx", c, p] = gx
+        def weigh(chunk, p):
+            message = work.tile([PART, TAGS], BF16, name=f"message_{p}", bufs=2, align_bytes=64)
+            nc.vector.scalar_tensor_tensor(
+                out=message[:],
+                in0=live.pop(("powers", chunk, 2 * p))[:],
+                scalar=stats[chunk][:, 8 + p : 9 + p],
+                in1=gain512[p][:],
+                op0=ALU.mult,
+                op1=ALU.mult,
+            )
+            live["message", chunk, p] = message
 
-        def vM(c, p):
-            v = work.tile([P, T], BF16, name="v", tag=f"v{p}", bufs=2, align_bytes=64)
-            if 2 * c + p in VG:
-                nc.scalar.activation(
-                    out=v[:], in_=st.pop(("gx", c, p))[:], func=ACT.Copy, scale=stats[c][:, 8 + p : 9 + p]
-                )
-            else:
-                nc.vector.scalar_tensor_tensor(
-                    out=v[:], in0=st.pop(("ex", (c, 2 * p)))[:], scalar=stats[c][:, 8 + p : 9 + p], in1=gain512[p][:],
-                    op0=ALU.mult, op1=ALU.mult,
-                )
-            st["v", c, p] = v
-
-        def vT(c):
-            vt = psum.tile([P, 2, 2, P], F32, name="vt", tag="xt", bufs=XB)
+        def turn_messages(chunk):
+            turned = psum.tile([PART, 2, 2, PART], F32, name="messages_turned", tag="turned", bufs=2)
             for p in range(2):
-                w = st.pop(("v", c, p))[:].bitcast(F32)
+                pairs = live.pop(("message", chunk, p))[:].bitcast(F32)
                 for h in range(2):
-                    nc.tensor.transpose(vt[:, p, h, :], w[:, h::2], ident[:])
-            st["vt", c] = vt
+                    nc.tensor.transpose(turned[:, p, h, :], pairs[:, h::2], ident[:])
+            live["messages_turned", chunk] = turned
 
-        def vC(c):
-            vg = work.tile([P, 2 * P * 4], BF16, name="vg", tag="vg", bufs=2, align_bytes=64)
-            eng = nc.scalar.copy if VCE == "S" else nc.vector.tensor_copy
-            eng(
-                out=vg[:].bitcast(F32).rearrange("p (g r h) -> p g r h", g=2, h=2),
-                in_=st.pop(("vt", c))[:].rearrange("p g h r -> p g r h"),
+        def copy_messages(chunk):
+            grouped = work.tile([PART, 2 * PART * PACK], BF16, name="messages_grouped", bufs=2, align_bytes=64)
+            nc.scalar.copy(
+                out=grouped[:].bitcast(F32).rearrange("p (m r h) -> p m r h", m=2, h=2),
+                in_=live.pop(("messages_turned", chunk))[:].rearrange("p m h r -> p m r h"),
             )
-            st["vg", c] = vg
+            live["messages_grouped", chunk] = grouped
 
-        def vQ(c):
-            vq = work.tile([P, 2, P], U32, name="vq", tag="vq", bufs=2, align_bytes=64)
-            vsc = work.tile([P, 2, P], U8, name="vsc", tag="vsc", bufs=2, align_bytes=64)
+        def quantise_messages(chunk):
+            codes = work.tile([PART, 2, PART], U32, name="message_codes", bufs=2, align_bytes=64)
+            scales = work.tile([PART, 2, PART], U8, name="message_scales", bufs=2, align_bytes=64)
             nc.vector.quantize_mx(
-                out=vq[:].rearrange("p g r -> p (g r)").bitcast(FP8X4),
-                scales=vsc[:].rearrange("p g r -> p (g r)"),
-                in_=st.pop(("vg", c))[:],
+                out=codes[:].rearrange("p m r -> p (m r)").bitcast(FP8X4),
+                scales=scales[:].rearrange("p m r -> p (m r)"),
+                in_=live.pop(("messages_grouped", chunk))[:],
             )
-            st["vq", c] = (vq, vsc)
+            live["message_codes", chunk] = (codes, scales)
 
-        def mM(c):
-            vq, vsc = st.pop(("vq", c))
+        def pass_messages(chunk):
+            codes, scales = live.pop(("message_codes", chunk))
             for p in range(2):
-                acc = psum.tile([P, T], F32, name="m", tag="m", bufs=MB)
+                acc = psum.tile([PART, TAGS], F32, name="passed", tag="passed", bufs=2)
                 nc.tensor.matmul_mx(
                     out=acc[:],
-                    lhsT=vq[:, p, :].bitcast(FP8X4), lhsT_scale=vsc[:, p, :],
-                    rhs=tcodes[:, p, :].bitcast(FP8X4), rhs_scale=tscale[:, p, :],
-                    start=True, stop=True,
+                    lhsT=codes[:, p, :].bitcast(FP8X4),
+                    lhsT_scale=scales[:, p, :],
+                    rhs=trans_codes[:, p, :].bitcast(FP8X4),
+                    rhs_scale=trans_scales[:, p, :],
+                    start=True,
+                    stop=True,
                 )
-                st["m", c, p] = acc
+                live["passed", chunk, p] = acc
 
-        def f0(c):
-            r0 = work.tile([P, T], F32, name="r0", tag="r0", bufs=2)
-            if c in ZG:
+        def floor_first(chunk):
+            above = work.tile([PART, TAGS], F32, name="above", bufs=2)
+            nc.scalar.activation(
+                out=above[:], in_=live.pop(("passed", chunk, 0))[:], func=ACT.Relu, bias=FLOOR, scale=1.0
+            )
+            live["above", chunk] = above
+
+        def floor_second(chunk):
+            floored = work.tile([PART, TAGS], F32, name="floored", bufs=2)
+            passed = live.pop(("passed", chunk, 1))
+            if chunk in SCALAR_FLOOR_CHUNKS:
+                relu = work.tile([PART, TAGS], F32, name="relu", bufs=2)
+                nc.scalar.activation(out=relu[:], in_=passed[:], func=ACT.Relu, bias=FLOOR, scale=1.0)
+                nc.scalar.activation(out=floored[:], in_=relu[:], func=ACT.Identity, bias=ABOVE, scale=1.0)
+            else:
                 nc.vector.tensor_scalar(
-                    out=r0[:], in0=st.pop(("m", c, 0))[:], scalar1=-14.4, scalar2=16.0, op0=ALU.max, op1=ALU.add
+                    out=floored[:], in0=passed[:], scalar1=-FLOOR, scalar2=16.0, op0=ALU.max, op1=ALU.add
                 )
-                st["r0", c] = r0
-                return
-            nc.scalar.activation(out=r0[:], in_=st.pop(("m", c, 0))[:], func=ACT.Relu, bias=14.4, scale=1.0)
-            st["r0", c] = r0
+            live["floored", chunk] = floored
 
-        def f1(c):
-            z1 = work.tile([P, T], F32, name="z1", tag="z1", bufs=2)
-            if c in W:
-                r1 = work.tile([P, T], F32, name="r1", tag="r1", bufs=2)
-                nc.scalar.activation(out=r1[:], in_=st.pop(("m", c, 1))[:], func=ACT.Relu, bias=14.4, scale=1.0)
-                for a in range(GSPLIT):
-                    k = slice(a * T // GSPLIT, (a + 1) * T // GSPLIT)
-                    nc.gpsimd.tensor_scalar(
-                        out=z1[:, k], in0=r1[:, k], scalar1=1.6, scalar2=1.0, op0=ALU.add, op1=ALU.mult
-                    )
-                st["z1", c] = z1
-                return
-            nc.vector.tensor_scalar(
-                out=z1[:], in0=st.pop(("m", c, 1))[:], scalar1=-14.4, scalar2=16.0, op0=ALU.max, op1=ALU.add
-            )
-            st["z1", c] = z1
-
-        def zP(c):
-            z = keep.tile([P, T], F32, name=f"z_{c}")
-            if c in ZG:
-                nc.gpsimd.tensor_tensor(out=z[:], in0=st.pop(("r0", c))[:], in1=st.pop(("z1", c))[:], op=ALU.mult)
-                st["z", c] = z
-                return
+        def multiply_floors(chunk):
+            product = keep.tile([PART, TAGS], F32, name=f"product_{chunk}")
             nc.vector.scalar_tensor_tensor(
-                out=z[:], in0=st.pop(("r0", c))[:], scalar=1.6, in1=st.pop(("z1", c))[:], op0=ALU.add, op1=ALU.mult
+                out=product[:],
+                in0=live.pop(("above", chunk))[:],
+                scalar=ABOVE,
+                in1=live.pop(("floored", chunk))[:],
+                op0=ALU.add,
+                op1=ALU.mult,
             )
-            st["z", c] = z
+            live["product_of_floors", chunk] = product
 
-        def zE(c):
-            s = stats[c]
-            ez = work.tile([P, T], F32, name="ez", tag="ez", bufs=2)
-            ex = st.pop(("ex", (c, 1)))
-            if c in EZG:
-                for a in range(GSPLIT):
-                    k = slice(a * T // GSPLIT, (a + 1) * T // GSPLIT)
-                    nc.gpsimd.tensor_tensor(out=ez[:, k], in0=ex[:, k], in1=st["z", c][:, k], op=ALU.mult)
-                st["ez", c] = ez
-            else:
-                nc.vector.scalar_tensor_tensor(
-                    out=ez[:], in0=ex[:], scalar=1.0 / 512, in1=st["z", c][:],
-                    op0=ALU.mult, op1=ALU.mult, accum_out=s[:, 10:11],
-                )
+        def sum_weighted(chunk):
+            weighted = work.tile([PART, TAGS], F32, name="weighted", bufs=2)
+            nc.vector.scalar_tensor_tensor(
+                out=weighted[:],
+                in0=live.pop(("powers", chunk, 1))[:],
+                scalar=1.0 / TAGS,
+                in1=live["product_of_floors", chunk][:],
+                op0=ALU.mult,
+                op1=ALU.mult,
+                accum_out=stats[chunk][:, 10:11],
+            )
 
-        def zA(c):
-            if c in EZG:
-                ez = st.pop(("ez", c))
-                nc.scalar.activation(
-                    out=ez[:], in_=ez[:], func=ACT.Copy, scale=1.0 / 512, accum_out=stats[c][:, 10:11]
-                )
+        def invert_total(chunk):
+            nc.vector.reciprocal(out=stats[chunk][:, 11:12], in_=stats[chunk][:, 10:11])
 
-        def zR(c):
-            s = stats[c]
-            nc.vector.reciprocal(out=s[:, 11:12], in_=s[:, 10:11])
+        def take_log(chunk):
+            logs = work.tile([PART, TAGS], F32, name="logs", bufs=3)
+            nc.scalar.activation(
+                out=logs[:], in_=live.pop(("product_of_floors", chunk))[:], func=ACT.Ln, scale=stats[chunk][:, 11:12]
+            )
+            live["logs", chunk] = logs
 
-        rcodes = keep.tile([P, TOKENS], U32, name="rcodes", align_bytes=64)
-        rscale = keep.tile([P, TOKENS], U8, name="rscale", align_bytes=64)
+        def finish_result(chunk):
+            result = work.tile([PART, TAGS], F32, name="result", bufs=4)
+            nc.vector.scalar_tensor_tensor(
+                out=result[:],
+                in0=live.pop(("logs", chunk))[:],
+                scalar=stats[chunk][:, 1:2],
+                in1=live.pop(("negated", chunk))[:],
+                op0=ALU.add,
+                op1=ALU.subtract,
+            )
+            nc.sync.dma_start(out=out_0[chunk * PART : (chunk + 1) * PART, :], in_=result[:])
+            live["result", chunk] = result
 
-        def rL(c):
-            lz = work.tile([P, T], F32, name="lz", tag="lz", bufs=3)
-            nc.scalar.activation(out=lz[:], in_=st.pop(("z", c))[:], func=ACT.Ln, scale=stats[c][:, 11:12])
-            st["lz", c] = lz
+        def turn_result(chunk):
+            turned = psum.tile([PART, PACK, PART], F32, name="result_turned", tag="turned", bufs=2)
+            result = live.pop(("result", chunk))
+            for t in range(PACK):
+                nc.tensor.transpose(turned[:, t, :], result[:, t::PACK], ident[:])
+            live["result_turned", chunk] = turned
 
-        def rA(c):
-            r = work.tile([P, T], F32, name="r", tag="r", bufs=4)
-            n, lz = st.pop(("n", (c, 1))), st.pop(("lz", c))
-            if True:
-                nc.vector.scalar_tensor_tensor(
-                    out=r[:], in0=lz[:], scalar=stats[c][:, 1:2], in1=n[:], op0=ALU.add, op1=ALU.subtract
-                )
-            else:
-                nc.vector.scalar_tensor_tensor(
-                    out=r[:], in0=n[:], scalar=stats[c][:, 1:2], in1=lz[:], op0=ALU.add, op1=ALU.add
-                )
-            nc.sync.dma_start(out=out_0[c * P : (c + 1) * P, :], in_=r[:])
-            st["r", c] = r
+        def copy_result(chunk):
+            if chunk % 2 == 0:
+                grouped = work.tile([PART, 2, PART, PACK], BF16, name="result_grouped", bufs=3, align_bytes=64)
+                live["result_grouped", chunk // 2] = grouped
+            nc.scalar.copy(
+                out=live["result_grouped", chunk // 2][:, chunk % 2, :, :],
+                in_=live.pop(("result_turned", chunk))[:].rearrange("p t r -> p r t"),
+            )
 
-        def rT(c):
-            rt = psum.tile([P, 4, P], F32, name="rt", tag="xt", bufs=XB)
-            r = st.pop(("r", c))
-            for j in range(4):
-                nc.tensor.transpose(rt[:, j, :], r[:, j::4], ident[:])
-            st["rt", c] = rt
-
-        def rC(c):
-            if c % 2 == 0:
-                rg = work.tile([P, 2, P, 4], BF16, name="rg", tag="rg", bufs=3, align_bytes=64)
-                st["rg", c // 2] = rg
-            eng = nc.vector.tensor_copy if c in VRC else nc.scalar.copy
-            eng(out=st["rg", c // 2][:, c % 2, :, :], in_=st.pop(("rt", c))[:].rearrange("p j r -> p r j"))
-
-        def rQ(c):
-            if c % 2 == 0:
+        def quantise_result(chunk):
+            if chunk % 2 == 0:
                 return
-            k = c // 2
-            cols = slice(2 * P * k, 2 * P * (k + 1))
+            cols = slice((chunk - 1) * PART, (chunk + 1) * PART)
             nc.vector.quantize_mx(
-                out=rcodes[:, cols].bitcast(FP8X4), scales=rscale[:, cols],
-                in_=st.pop(("rg", k))[:].rearrange("p c r j -> p (c r j)"),
+                out=result_codes[:, cols].bitcast(FP8X4),
+                scales=result_scales[:, cols],
+                in_=live.pop(("result_grouped", chunk // 2))[:].rearrange("p c r t -> p (c r t)"),
             )
             nc.sync.dma_start(
-                out=out_1[0, :, cols, :].rearrange("p m t -> p (m t)").bitcast(I32), in_=rcodes[:, cols].bitcast(I32)
+                out=out_1[0, :, cols, :].rearrange("p m t -> p (m t)").bitcast(I32),
+                in_=result_codes[:, cols].bitcast(I32),
             )
 
-        v0 = lambda f: (lambda c: f(c, 0))
-        v1 = lambda f: (lambda c: f(c, 1))
-        v3 = lambda f, i: (lambda c: f(i))
-        ops = {
-            "eN": eN, "kB0": v3(kB, 2), "kB1": v3(kB, 0), "kG0": v3(kG, 0), "kG1": v3(kG, 1), "tI": tI, "tQ": tQ, "xT": xT, "xC": xC, "xQ": xQ, "eM": eM, "eS": eS, "eT": eT,
-            "eX": eX, "eE": eE, "vR": vR, "vG0": v0(vG), "vG1": v1(vG), "vM0": v0(vM), "vM1": v1(vM),
-            "vT": vT, "vC": vC, "vQ": vQ, "mM": mM, "f0": f0, "f1": f1, "zP": zP, "zE": zE, "zA": zA, "zR": zR,
-            "rL": rL, "rA": rA, "rT": rT, "rC": rC, "rQ": rQ,
+        steps = {
+            "spread_bias_0": lambda i: spread_bias(0),
+            "spread_bias_2": lambda i: spread_bias(2),
+            "spread_gain_0": lambda i: spread_gain(0),
+            "spread_gain_1": lambda i: spread_gain(1),
+            "interleave_trans_0a": lambda i: interleave_trans(0, 0),
+            "interleave_trans_0b": lambda i: interleave_trans(0, 1),
+            "interleave_trans_1a": lambda i: interleave_trans(1, 0),
+            "interleave_trans_1b": lambda i: interleave_trans(1, 1),
+            "quantise_trans_0": lambda i: quantise_trans(0),
+            "quantise_trans_1": lambda i: quantise_trans(1),
+            "turn_x": turn_x,
+            "copy_x": copy_x,
+            "quantise_x": quantise_x,
+            "multiply_x": multiply_x,
+            "save_scores": save_scores,
+            "return_scores": return_scores,
+            "add_bias": add_bias,
+            "find_maximum": find_maximum,
+            "exponentiate": exponentiate,
+            "invert_sums": invert_sums,
+            "weigh_first": lambda chunk: weigh(chunk, 0),
+            "weigh_second": lambda chunk: weigh(chunk, 1),
+            "turn_messages": turn_messages,
+            "copy_messages": copy_messages,
+            "quantise_messages": quantise_messages,
+            "pass_messages": pass_messages,
+            "floor_first": floor_first,
+            "floor_second": floor_second,
+            "multiply_floors": multiply_floors,
+            "sum_weighted": sum_weighted,
+            "invert_total": invert_total,
+            "take_log": take_log,
+            "finish_result": finish_result,
+            "turn_result": turn_result,
+            "copy_result": copy_result,
+            "quantise_result": quantise_result,
         }
-        count = {"u": len(units), "c": CHUNKS, "t": CHUNKS, "k": 1, "g": 2, "i": 4, "q": 2}
-        for s in range(60):
-            for op, kind, lag in ORDER:
-                j = s - lag
-                if kind == "c":
-                    if j % 3:
-                        continue
-                    j = j // 3
-                if 0 <= j < count[kind]:
-                    ops[op](j)
-        for q in range(4):
+        stride = {"tile": 1, "chunk": LAYERS, "tail": 1, "once": 1}
+        count = {"tile": len(tiles), "chunk": CHUNKS, "tail": CHUNKS, "once": 1}
+        last = max(lag + stride[kind] * (count[kind] - 1) for name, kind, lag in ISSUE_ORDER)
+        for s in range(last + 1):
+            for name, kind, lag in ISSUE_ORDER:
+                index, rest = divmod(s - lag, stride[kind])
+                if rest == 0 and 0 <= index < count[kind]:
+                    steps[name](index)
+
+        for quadrant in range(4):
             nc.sync.dma_start(
-                out=out_2[0, 4 * q : 4 * q + 4, :].bitcast(I32),
-                in_=rscale[32 * q : 32 * q + 4, :].bitcast(I32),
+                out=out_2[0, 4 * quadrant : 4 * quadrant + 4, :].bitcast(I32),
+                in_=result_scales[32 * quadrant : 32 * quadrant + 4, :].bitcast(I32),
             )

from contextlib import ExitStack

import concourse.mybir as mybir
from concourse.masks import make_identity

F32 = mybir.dt.float32
BF16 = mybir.dt.bfloat16
I32 = mybir.dt.int32
U32 = mybir.dt.uint32
U8 = mybir.dt.uint8
FP8X4 = mybir.dt.float8_e4m3fn_x4
FP4X4 = mybir.dt.float4_e2m1fn_x4
ALU = mybir.AluOpType
ACT = mybir.ActivationFunctionType
AXIS = mybir.AxisListType

LAYERS, TOKENS, D, TAGS = 3, 1024, 1024, 512
PART = 128
CHUNKS = TOKENS // PART
PASSES = D // 512
PACK = 4
QUARTERS = TAGS // PART
FLOPS = 2 * LAYERS * TOKENS * D * TAGS + 2 * 2 * TOKENS * TAGS * TAGS

FLOOR = 14.4
ABOVE = 1.6

LAYER_ORDER = (0, 2, 1)
BIAS_ROW = {0: 0, 2: 1, 1: 2}
TRANS_BEFORE = (2, 3)

ISSUE_ORDER = (
    ("pass_messages", "chunk", 10),
    ("save_scores", "tile", 2),
    ("quantise_trans_0", "once", 9),
    ("quantise_trans_1", "once", 5),
    ("quantise_x", "tile", 1),
    ("add_bias", "tile", 2),
    ("interleave_trans_1b", "once", 4),
    ("spread_bias_0", "once", 1),
    ("spread_gain_1", "once", 1),
    ("take_log", "tail", 28),
    ("floor_second", "chunk", 11),
    ("exponentiate", "tile", 4),
    ("copy_result", "tail", 31),
    ("turn_x", "tile", 0),
    ("quantise_messages", "chunk", 9),
    ("interleave_trans_0b", "once", 2),
    ("find_maximum", "tile", 3),
    ("spread_bias_2", "once", 0),
    ("invert_total", "chunk", 13),
    ("copy_x", "tile", 0),
    ("turn_messages", "chunk", 8),
    ("weigh_first", "chunk", 7),
    ("turn_result", "tail", 30),
    ("interleave_trans_1a", "once", 2),
    ("multiply_x", "tile", 1),
    ("invert_sums", "chunk", 6),
    ("sum_weighted", "chunk", 12),
    ("weigh_second", "chunk", 7),
    ("copy_messages", "chunk", 8),
    ("return_scores", "tile", 2),
    ("quantise_result", "tail", 35),
    ("spread_gain_0", "once", 2),
    ("finish_result", "tail", 29),
    ("multiply_floors", "chunk", 11),
    ("floor_first", "chunk", 10),
    ("interleave_trans_0a", "once", 4),
)


TENSOR_BIAS_CHUNKS = (2, 4, 6)
SCALAR_FLOOR_CHUNKS = (2, 4)


def bias_on_tensor(chunk, layer):
    return layer == 1 or (layer == 0 and chunk in TENSOR_BIAS_CHUNKS)


def tile_chunkflooredmessagemiddlescore_kernel(
    tc, x, we_words, we_scales, be, ends, gain, trans, out_0, out_1, out_2
):
    nc = tc.nc
    with ExitStack() as ctx:
        keep = ctx.enter_context(tc.tile_pool(name="keep", bufs=1))
        work = ctx.enter_context(tc.tile_pool(name="work", bufs=3))
        psum = ctx.enter_context(tc.psum_pool(name="psum", bufs=2))
        ctx.enter_context(tc.manual_schedule())

        x_tiles = {}
        words = keep.tile([PART, PASSES, 2 * TAGS], U8, name="we_words", align_bytes=64)
        word_scales = keep.tile([PART, PASSES, TAGS], U8, name="we_scales", align_bytes=64)
        rows = keep.tile([PART, 5, TAGS], BF16, name="rows", align_bytes=64)
        ones = keep.tile([PART, PART], BF16, name="ones", align_bytes=64)
        ident = keep.tile([PART, PART], F32, name="ident")
        make_identity(nc, ident[:])
        nc.vector.memset(rows[:, 0:3, :], 0.0)
        nc.vector.memset(word_scales[:].rearrange("p g n -> p (g n)").bitcast(I32), 0)
        nc.vector.memset(ones[:], 0.0)
        nc.vector.memset(rows[:, 3:5, :], 0.0)

        def load_x(chunk, layer):
            tile = keep.tile([PART, D], BF16, name=f"x_{chunk}_{layer}", align_bytes=64)
            nc.sync.dma_start(out=tile[:], in_=x[layer, chunk * PART : (chunk + 1) * PART, :])
            x_tiles[chunk, layer] = tile

        def as_words(ap):
            return ap.rearrange("p g n -> p (g n)").bitcast(I32).rearrange("p (g n) -> p g n", g=PASSES)

        tiles = [(chunk, layer) for chunk in range(CHUNKS) for layer in LAYER_ORDER]
        load_x(*tiles[0])
        nc.sync.dma_start(out=as_words(words[:]), in_=we_words.bitcast(I32).rearrange("g p n -> p g n"))
        for quadrant in range(4):
            nc.sync.dma_start(
                out=as_words(word_scales[32 * quadrant : 32 * quadrant + 4, :, :]),
                in_=we_scales[:, 4 * quadrant : 4 * quadrant + 4, :].bitcast(I32).rearrange("g r n -> r g n"),
            )
        nc.scalar.dma_start(
            out=rows[0:1, 0:3, :], in_=be.unsqueeze(0).unsqueeze(0).to_broadcast([1, 3, TAGS])
        )
        nc.scalar.dma_start(out=rows[1:2, 0:2, :], in_=ends.unsqueeze(0))
        nc.scalar.dma_start(out=rows[0:1, 3:5, :], in_=gain.unsqueeze(0))
        trans_raw = {}
        for place, tile_id in enumerate(tiles[1:]):
            for p in range(2):
                if place == TRANS_BEFORE[p]:
                    raw = keep.tile([PART, PACK, TAGS], BF16, name=f"trans_raw_{p}", align_bytes=64)
                    nc.sync.dma_start(out=raw[:], in_=trans[p].rearrange("(k j) n -> k j n", j=PACK))
                    trans_raw[p] = raw
            load_x(*tile_id)
        nc.scalar.activation(out=ones[:], in_=ones[:], func=ACT.Exp)

        trans_codes = keep.tile([PART, 2, TAGS], U32, name="trans_codes", align_bytes=64)
        trans_scales = keep.tile([PART, 2, TAGS], U8, name="trans_scales", align_bytes=64)
        trans_grouped = []
        for p in range(2):
            grouped = keep.tile([PART, TAGS, PACK], BF16, name=f"trans_grouped_{p}", align_bytes=64)
            trans_grouped.append(grouped)
        stats = []
        for chunk in range(CHUNKS):
            columns = keep.tile([PART, 16], F32, name=f"stats_{chunk}")
            stats.append(columns)
        result_codes = keep.tile([PART, TOKENS], U32, name="result_codes", align_bytes=64)
        result_scales = keep.tile([PART, TOKENS], U8, name="result_scales", align_bytes=64)
        bias = {}
        gain512 = {}
        live = {}

        def spread(block, tag, bufs):
            acc = psum.tile([PART, TAGS], F32, name="spread", tag=tag, bufs=bufs)
            nc.tensor.matmul(acc[:], lhsT=ones[:], rhs=rows[:, block, :], start=True, stop=True)
            return acc

        def spread_bias(layer):
            acc = spread(BIAS_ROW[layer], "scores", 3)
            full = keep.tile([PART, TAGS], F32, name=f"bias_{layer}")
            nc.vector.tensor_copy(out=full[:], in_=acc[:])
            bias[layer] = full

        def spread_gain(p):
            acc = spread(3 + p, "passed", 2)
            full = keep.tile([PART, TAGS], F32, name=f"gain512_{p}")
            nc.scalar.activation(out=full[:], in_=acc[:], func=ACT.Copy, scale=512.0)
            gain512[p] = full

        def interleave_trans(p, half):
            cols = slice(half * TAGS // 2, (half + 1) * TAGS // 2)
            nc.vector.tensor_copy(
                out=trans_grouped[p][:, cols, :], in_=trans_raw[p][:, :, cols].rearrange("k j n -> k n j")
            )

        def quantise_trans(p):
            nc.vector.quantize_mx(
                out=trans_codes[:, p, :].bitcast(FP8X4),
                scales=trans_scales[:, p, :],
                in_=trans_grouped[p][:].rearrange("k n j -> k (n j)"),
            )

        def turn_x(tile):
            turned = psum.tile([PART, PASSES, 2, PART], F32, name="x_turned", tag="turned", bufs=2)
            pairs = x_tiles[tiles[tile]][:].bitcast(F32)
            for g in range(PASSES):
                for h in range(2):
                    nc.tensor.transpose(turned[:, g, h, :], pairs[:, 256 * g + h : 256 * (g + 1) : 2], ident[:])
            live["x_turned", tile] = turned

        def copy_x(tile):
            grouped = work.tile([PART, PASSES * PART * PACK], BF16, name="x_grouped", bufs=3, align_bytes=64)
            nc.scalar.copy(
                out=grouped[:].bitcast(F32).rearrange("p (g r h) -> p g r h", g=PASSES, h=2),
                in_=live.pop(("x_turned", tile))[:].rearrange("p g h r -> p g r h"),
            )
            live["x_grouped", tile] = grouped

        def quantise_x(tile):
            codes = work.tile([PART, PASSES, PART], U32, name="x_codes", bufs=3, align_bytes=64)
            scales = work.tile([PART, PASSES, PART], U8, name="x_scales", bufs=3, align_bytes=64)
            nc.vector.quantize_mx(
                out=codes[:].rearrange("p g r -> p (g r)").bitcast(FP8X4),
                scales=scales[:].rearrange("p g r -> p (g r)"),
                in_=live.pop(("x_grouped", tile))[:],
            )
            live["x_codes", tile] = (codes, scales)

        def multiply_x(tile):
            codes, scales = live.pop(("x_codes", tile))
            if bias_on_tensor(*tiles[tile]):
                acc = psum.tile([PART, QUARTERS, PART], F32, name="flipped", tag="flipped", bufs=1)
                for q in range(QUARTERS):
                    for g in range(PASSES):
                        nc.tensor.matmul_mx(
                            out=acc[:, q, :],
                            lhsT=words[:, g, 2 * PART * q : 2 * PART * (q + 1)].bitcast(FP4X4),
                            lhsT_scale=word_scales[:, g, PART * q : PART * (q + 1)],
                            rhs=codes[:, g, :].bitcast(FP8X4),
                            rhs_scale=scales[:, g, :],
                            start=g == 0,
                            stop=g == PASSES - 1,
                        )
            else:
                acc = psum.tile([PART, TAGS], F32, name="scores", tag="scores", bufs=3)
                for g in range(PASSES):
                    nc.tensor.matmul_mx(
                        out=acc[:],
                        lhsT=codes[:, g, :].bitcast(FP8X4),
                        lhsT_scale=scales[:, g, :],
                        rhs=words[:, g, :].bitcast(FP4X4),
                        rhs_scale=word_scales[:, g, :],
                        start=g == 0,
                        stop=g == PASSES - 1,
                    )
            live["product", tile] = acc

        def save_scores(tile):
            if not bias_on_tensor(*tiles[tile]):
                return
            saved = work.tile([PART, QUARTERS, PART], F32, name="saved", bufs=2)
            nc.scalar.copy(out=saved[:], in_=live.pop(("product", tile))[:])
            live["saved", tile] = saved

        def return_scores(tile):
            if not bias_on_tensor(*tiles[tile]):
                return
            saved = live.pop(("saved", tile))
            acc = psum.tile([PART, TAGS], F32, name="scores", tag="scores", bufs=3)
            block = BIAS_ROW[tiles[tile][1]]
            nc.tensor.matmul(acc[:], lhsT=ones[:], rhs=rows[:, block, :], start=True, stop=False)
            for q in range(QUARTERS):
                nc.tensor.matmul(
                    acc[:, PART * q : PART * (q + 1)],
                    lhsT=saved[:, q, :],
                    rhs=ident[:],
                    start=False,
                    stop=q == QUARTERS - 1,
                    is_transpose=True,
                )
            live["biased", tile] = acc

        def add_bias(tile):
            if bias_on_tensor(*tiles[tile]):
                return
            biased = work.tile([PART, TAGS], F32, name="biased", bufs=3)
            nc.vector.tensor_tensor(
                out=biased[:], in0=live.pop(("product", tile))[:], in1=bias[tiles[tile][1]][:], op=ALU.add
            )
            live["biased", tile] = biased

        def find_maximum(tile):
            chunk, layer = tiles[tile]
            biased = live.pop(("biased", tile))
            column = stats[chunk][:, layer : layer + 1]
            if layer == 1:
                negated = keep.tile([PART, TAGS], F32, name=f"negated_{chunk}")
                nc.vector.tensor_scalar(
                    out=negated[:],
                    in0=biased[:],
                    scalar1=-1.0,
                    scalar2=None,
                    op0=ALU.mult,
                    op1=ALU.min,
                    accum_out=column,
                )
                live["negated", chunk] = negated
            else:
                nc.vector.tensor_reduce(out=column, in_=biased[:], axis=AXIS.X, op=ALU.max, negate=True)
                live["scores", tile] = biased

        def exponentiate(tile):
            chunk, layer = tiles[tile]
            column = stats[chunk][:, layer : layer + 1]
            powers = work.tile([PART, TAGS], F32, name=f"powers_{layer}", bufs=3)
            if layer == 1:
                nc.scalar.activation(
                    out=powers[:], in_=live["negated", chunk][:], func=ACT.Exp, bias=column, scale=-1.0
                )
            else:
                p = layer // 2
                nc.scalar.activation(
                    out=powers[:],
                    in_=live.pop(("scores", tile))[:],
                    func=ACT.Exp,
                    bias=column,
                    scale=1.0,
                    accum_out=stats[chunk][:, 4 + p : 5 + p],
                )
            live["powers", chunk, layer] = powers

        def invert_sums(chunk):
            nc.vector.reciprocal(out=stats[chunk][:, 8:10], in_=stats[chunk][:, 4:6])

        def weigh(chunk, p):
            message = work.tile([PART, TAGS], BF16, name=f"message_{p}", bufs=2, align_bytes=64)
            nc.vector.scalar_tensor_tensor(
                out=message[:],
                in0=live.pop(("powers", chunk, 2 * p))[:],
                scalar=stats[chunk][:, 8 + p : 9 + p],
                in1=gain512[p][:],
                op0=ALU.mult,
                op1=ALU.mult,
            )
            live["message", chunk, p] = message

        def turn_messages(chunk):
            turned = psum.tile([PART, 2, 2, PART], F32, name="messages_turned", tag="turned", bufs=2)
            for p in range(2):
                pairs = live.pop(("message", chunk, p))[:].bitcast(F32)
                for h in range(2):
                    nc.tensor.transpose(turned[:, p, h, :], pairs[:, h::2], ident[:])
            live["messages_turned", chunk] = turned

        def copy_messages(chunk):
            grouped = work.tile([PART, 2 * PART * PACK], BF16, name="messages_grouped", bufs=2, align_bytes=64)
            nc.scalar.copy(
                out=grouped[:].bitcast(F32).rearrange("p (m r h) -> p m r h", m=2, h=2),
                in_=live.pop(("messages_turned", chunk))[:].rearrange("p m h r -> p m r h"),
            )
            live["messages_grouped", chunk] = grouped

        def quantise_messages(chunk):
            codes = work.tile([PART, 2, PART], U32, name="message_codes", bufs=2, align_bytes=64)
            scales = work.tile([PART, 2, PART], U8, name="message_scales", bufs=2, align_bytes=64)
            nc.vector.quantize_mx(
                out=codes[:].rearrange("p m r -> p (m r)").bitcast(FP8X4),
                scales=scales[:].rearrange("p m r -> p (m r)"),
                in_=live.pop(("messages_grouped", chunk))[:],
            )
            live["message_codes", chunk] = (codes, scales)

        def pass_messages(chunk):
            codes, scales = live.pop(("message_codes", chunk))
            for p in range(2):
                acc = psum.tile([PART, TAGS], F32, name="passed", tag="passed", bufs=2)
                nc.tensor.matmul_mx(
                    out=acc[:],
                    lhsT=codes[:, p, :].bitcast(FP8X4),
                    lhsT_scale=scales[:, p, :],
                    rhs=trans_codes[:, p, :].bitcast(FP8X4),
                    rhs_scale=trans_scales[:, p, :],
                    start=True,
                    stop=True,
                )
                live["passed", chunk, p] = acc

        def floor_first(chunk):
            above = work.tile([PART, TAGS], F32, name="above", bufs=2)
            nc.scalar.activation(
                out=above[:], in_=live.pop(("passed", chunk, 0))[:], func=ACT.Relu, bias=FLOOR, scale=1.0
            )
            live["above", chunk] = above

        def floor_second(chunk):
            floored = work.tile([PART, TAGS], F32, name="floored", bufs=2)
            passed = live.pop(("passed", chunk, 1))
            if chunk in SCALAR_FLOOR_CHUNKS:
                relu = work.tile([PART, TAGS], F32, name="relu", bufs=2)
                nc.scalar.activation(out=relu[:], in_=passed[:], func=ACT.Relu, bias=FLOOR, scale=1.0)
                nc.scalar.activation(out=floored[:], in_=relu[:], func=ACT.Identity, bias=ABOVE, scale=1.0)
            else:
                nc.vector.tensor_scalar(
                    out=floored[:], in0=passed[:], scalar1=-FLOOR, scalar2=16.0, op0=ALU.max, op1=ALU.add
                )
            live["floored", chunk] = floored

        def multiply_floors(chunk):
            product = keep.tile([PART, TAGS], F32, name=f"product_{chunk}")
            nc.vector.scalar_tensor_tensor(
                out=product[:],
                in0=live.pop(("above", chunk))[:],
                scalar=ABOVE,
                in1=live.pop(("floored", chunk))[:],
                op0=ALU.add,
                op1=ALU.mult,
            )
            live["product_of_floors", chunk] = product

        def sum_weighted(chunk):
            weighted = work.tile([PART, TAGS], F32, name="weighted", bufs=2)
            nc.vector.scalar_tensor_tensor(
                out=weighted[:],
                in0=live.pop(("powers", chunk, 1))[:],
                scalar=1.0 / TAGS,
                in1=live["product_of_floors", chunk][:],
                op0=ALU.mult,
                op1=ALU.mult,
                accum_out=stats[chunk][:, 10:11],
            )

        def invert_total(chunk):
            nc.vector.reciprocal(out=stats[chunk][:, 11:12], in_=stats[chunk][:, 10:11])

        def take_log(chunk):
            logs = work.tile([PART, TAGS], F32, name="logs", bufs=3)
            nc.scalar.activation(
                out=logs[:], in_=live.pop(("product_of_floors", chunk))[:], func=ACT.Ln, scale=stats[chunk][:, 11:12]
            )
            live["logs", chunk] = logs

        def finish_result(chunk):
            result = work.tile([PART, TAGS], F32, name="result", bufs=4)
            nc.vector.scalar_tensor_tensor(
                out=result[:],
                in0=live.pop(("logs", chunk))[:],
                scalar=stats[chunk][:, 1:2],
                in1=live.pop(("negated", chunk))[:],
                op0=ALU.add,
                op1=ALU.subtract,
            )
            nc.sync.dma_start(out=out_0[chunk * PART : (chunk + 1) * PART, :], in_=result[:])
            live["result", chunk] = result

        def turn_result(chunk):
            turned = psum.tile([PART, PACK, PART], F32, name="result_turned", tag="turned", bufs=2)
            result = live.pop(("result", chunk))
            for t in range(PACK):
                nc.tensor.transpose(turned[:, t, :], result[:, t::PACK], ident[:])
            live["result_turned", chunk] = turned

        def copy_result(chunk):
            if chunk % 2 == 0:
                grouped = work.tile([PART, 2, PART, PACK], BF16, name="result_grouped", bufs=3, align_bytes=64)
                live["result_grouped", chunk // 2] = grouped
            nc.scalar.copy(
                out=live["result_grouped", chunk // 2][:, chunk % 2, :, :],
                in_=live.pop(("result_turned", chunk))[:].rearrange("p t r -> p r t"),
            )

        def quantise_result(chunk):
            if chunk % 2 == 0:
                return
            cols = slice((chunk - 1) * PART, (chunk + 1) * PART)
            nc.vector.quantize_mx(
                out=result_codes[:, cols].bitcast(FP8X4),
                scales=result_scales[:, cols],
                in_=live.pop(("result_grouped", chunk // 2))[:].rearrange("p c r t -> p (c r t)"),
            )
            nc.sync.dma_start(
                out=out_1[0, :, cols, :].rearrange("p m t -> p (m t)").bitcast(I32),
                in_=result_codes[:, cols].bitcast(I32),
            )

        steps = {
            "spread_bias_0": lambda i: spread_bias(0),
            "spread_bias_2": lambda i: spread_bias(2),
            "spread_gain_0": lambda i: spread_gain(0),
            "spread_gain_1": lambda i: spread_gain(1),
            "interleave_trans_0a": lambda i: interleave_trans(0, 0),
            "interleave_trans_0b": lambda i: interleave_trans(0, 1),
            "interleave_trans_1a": lambda i: interleave_trans(1, 0),
            "interleave_trans_1b": lambda i: interleave_trans(1, 1),
            "quantise_trans_0": lambda i: quantise_trans(0),
            "quantise_trans_1": lambda i: quantise_trans(1),
            "turn_x": turn_x,
            "copy_x": copy_x,
            "quantise_x": quantise_x,
            "multiply_x": multiply_x,
            "save_scores": save_scores,
            "return_scores": return_scores,
            "add_bias": add_bias,
            "find_maximum": find_maximum,
            "exponentiate": exponentiate,
            "invert_sums": invert_sums,
            "weigh_first": lambda chunk: weigh(chunk, 0),
            "weigh_second": lambda chunk: weigh(chunk, 1),
            "turn_messages": turn_messages,
            "copy_messages": copy_messages,
            "quantise_messages": quantise_messages,
            "pass_messages": pass_messages,
            "floor_first": floor_first,
            "floor_second": floor_second,
            "multiply_floors": multiply_floors,
            "sum_weighted": sum_weighted,
            "invert_total": invert_total,
            "take_log": take_log,
            "finish_result": finish_result,
            "turn_result": turn_result,
            "copy_result": copy_result,
            "quantise_result": quantise_result,
        }
        stride = {"tile": 1, "chunk": LAYERS, "tail": 1, "once": 1}
        count = {"tile": len(tiles), "chunk": CHUNKS, "tail": CHUNKS, "once": 1}
        last = max(lag + stride[kind] * (count[kind] - 1) for name, kind, lag in ISSUE_ORDER)
        for s in range(last + 1):
            for name, kind, lag in ISSUE_ORDER:
                index, rest = divmod(s - lag, stride[kind])
                if rest == 0 and 0 <= index < count[kind]:
                    steps[name](index)

        for quadrant in range(4):
            nc.sync.dma_start(
                out=out_2[0, 4 * quadrant : 4 * quadrant + 4, :].bitcast(I32),
                in_=result_scales[32 * quadrant : 32 * quadrant + 4, :].bitcast(I32),
            )
